import numpy as np
CORES = [40,64,80,88,96,104,120,144]
N = 8
R, T, B, CAPP = 4096, 2048, 32, 512
LOW = np.float32(-201 * 2.0 ** 92)
def entries(a): return a.T.reshape(-1)
def pack(v, P): return np.ascontiguousarray(np.asarray(v, np.int32).reshape(-1, P).T)
def table(rng, how, c=()):
    t = rng.standard_normal((N, 128, R), dtype=np.float32); k = np.arange(128) if how == "neg" else rng.permutation(128)[:16]
    t[:, k] = -0.125 - np.abs(t[:, k])
    if len(c): t[(c // R)[:, None], rng.permutation(128)[:16][None, :], (c % R)[:, None]] = LOW
    return t
def lists(rng, how):
    O = np.stack([rng.permutation(np.repeat(np.arange(N), CAPP))[:T] for r in range(N)])
    if how in ("astride", "early"): P = rng.permutation(N)[:T // CAPP]; O = np.stack([rng.permutation(np.repeat(P, CAPP)) for r in range(N)])
    I = R * O + rng.integers(0, R, (N, T))
    if how == "late": u = rng.random((N, T)); I = np.where(u < 0.5, R * O + np.where(u < 0.25, 0, R - 1), I)
    s = np.concatenate([[0], rng.integers(1 - T // 2, T // 2 + 1, N - 1), [int(rng.integers(1 - T // 2, 1))]])
    if how == "astride":
        z = int(rng.integers(1, N - 1)); k = int(rng.integers(0, B - 1)); s[1:z] = -rng.integers(1, T, z - 1); s[z] = -T; s[z + 1] = T; s[z + 2:N] = rng.integers(1, T, N - z - 2); s[N] = 0
    if how == "early": s[1:] = -T
    if how == "late": s[1:N] = T; s[N] = 0
    if how == "void":
        w = int(rng.integers(3, N - 1)); z = int(rng.integers(1, w - 1)); s[z] = int(rng.integers(1, T // 2 + 1)); s[z + 1] = s[z] - T; s[w:] = s[w] - T * np.arange(N + 1 - w)
    S = T * np.arange(N + 1) + s
    E = np.concatenate([np.append(np.sort(rng.integers(S[q], S[q + 1] + 1, B - 1)), S[q + 1]) for q in range(N)])
    if how == "astride":
        E[B * z:B * z + B - 1] = np.concatenate([np.sort(rng.integers(S[z], T * z - T // 2 + 1, k)), np.sort(rng.integers(T * z + T + T // 2, S[z + 1], B - 2 - k)), [S[z + 1] - 1]])
        L = max(N * T - 1, S[N - 1]); E[N * B - B:N * B - 1] = np.minimum(E[N * B - B:N * B - 1], L); E[N * B - 2] = L
        E += np.isin(E, np.setdiff1d(T * np.arange(1, N), S[z:z + 2]))
    if how == "neg":
        K = rng.random(N * B) < 0.5; K[0] = False; K[B - 1::B] = True; j = np.flatnonzero(K); E = E[j[np.searchsorted(j, np.arange(N * B))]]
    if how == "void":
        k = np.sort(np.stack([B * q + 1 + rng.permutation(B - 2)[:3] for q in range(N)]), axis=1); v = E[k]; v[:, 2] = S[1:]
        E = np.concatenate([[0], v.reshape(-1)])[np.searchsorted(k.reshape(-1), np.arange(N * B), side="right")]
    d = {"idx": np.stack([pack(i, 16) for i in I]), "end": np.stack([pack(E, 16)] * N)}
    if how == "neg":
        n = np.diff(np.concatenate([[0], E])).reshape(N, B); b = B * np.arange(N) + ((n > 0) * (1 + rng.random((N, B)))).argmax(axis=1)
        d["tab"] = table(rng, "neg", I.reshape(-1)[np.isin(np.searchsorted(E, np.arange(N * T), side="right"), b)])
    return d
def setup_inputs(rng):
    return dict({"tab": table(rng, "uniform")}, **lists(rng, "uniform"))
def setup_inputs_astride(rng):
    d = setup_inputs(rng); d.update(lists(rng, "astride"))
    for k in ("tab",): d[k] = (d[k].astype(np.float32) * 1048576.0).astype(d[k].dtype)
    return d
def setup_inputs_early(rng):
    d = setup_inputs(rng); d.update(lists(rng, "early"))
    for k in ("tab",): d[k] = (d[k].astype(np.float32) * (1 / 1024.0)).astype(d[k].dtype)
    return d
def setup_inputs_late(rng):
    d = setup_inputs(rng); d.update(lists(rng, "late"))
    return d
def setup_inputs_neg(rng):
    d = setup_inputs(rng); d.update(lists(rng, "neg"))
    return d
def setup_inputs_void(rng):
    d = setup_inputs(rng); d.update(lists(rng, "void"))
    return d
def check_inputs(x):
    bad = []
    if x["idx"].min() < 0 or x["idx"].max() >= N * R: bad.append("idx out of range")
    if x["end"].min() < 0 or x["end"].max() >= N * T + 1: bad.append("end out of range")
    if (x["end"] != x["end"][:1]).any(): bad.append("end differs from rank to rank")
    v = entries(x["end"][0]).astype(np.int64); s = v[B - 1::B]
    if (np.diff(v) < 0).any(): bad.append("end falls")
    if any(s[q - 1] > T * (q + 1) or (s[q - 1] < T * (q - 1) and s[q - 1] != s[N - 1]) for q in range(1, N)): bad.append("an entry belongs to a bag of a rank that is more than one away from its holder")
    if max(int(np.bincount(entries(a) // R, minlength=N).max()) for a in x["idx"]) > CAPP: bad.append("more than CAPP entries of a rank's idx point into one rank's part of the table")
    t = x["tab"].astype(np.float32)
    if t.min() < np.float32(-1e30) or t.max() > np.float32(1e30): bad.append("tab beyond -1e30 to 1e30")
    return bad
def reference(tab, idx, end):
    A = np.concatenate(list(tab), axis=1)
    G = A[:, np.concatenate([entries(a) for a in idx])]
    Y = np.zeros((128, N * B), tab.dtype)
    for r in range(N):
        c = np.concatenate([[0], entries(end[r])])
        for b in range(B * r, B * r + B):
            if c[b + 1] > c[b]: Y[:, b] = G[:, c[b]:c[b + 1]].max(axis=1)
    return {"y": np.stack([Y[:, B * r:B * r + B] for r in range(N)])}

@@ -1,0 +1,309 @@
+from concourse.bass import DstId, RemoteDMATransfer
+from concourse.mybir import AluOpType, ActivationFunctionType
+
+N, R, E, B = 8, 4096, 2048, 32
+HA = [0, 1, 2, 3, 4]
+HB = [7, 6, 5]
+W0 = 4
+VG = 256
+NEV = 132
+
+SCRATCH = {"F0": ("psum", [128, E], "float32"), "F1": ("psum", [128, E], "float32")}
+for _t, _l in (("float32", dict(win=R + 8, E8=72, DI=128, KI=96, CREP=128, CSH=128, CWR=128, TK=576, FW=8, PVS=64, GT=64,
+                                XO=64, ACC=256, RL=192, RES=256, M1=128, M2=64, M3=32, M4=32, YO=32, C1=2, NEG=1, POS=1,
+                                THR=1, X0=E, X1=E, X2=E, Y0=E + 1, Y1=E + 1)),
+               ("int32", dict(IDXI=128, IOI=512, EP=24)),
+               ("uint16", dict(IDX=1024, OFF=1024, IOT=E, XU=64)),
+               ("bfloat16", dict(NB0=128, NB=128, OH0=E, OH1=E, OH2=E, OH3=E, OH4=E))):
+    for _n, _w in _l.items():
+        SCRATCH[_n] = ("sbuf", [128, _w], _t)
+SEMAPHORES = (["l%d" % h for h in range(N)] + ["res", "tab", "endm", "rel1", "rel2", "lsem", "go"]
+              + ["e%d" % k for k in range(NEV)])
+
+
+def bits(m):
+    return [b for b in range(16) if (m >> b) & 1]
+
+
+def split(mask, n):
+    bb = bits(mask)
+    k = 1
+    while k * 2 * n <= len(bb):
+        k *= 2
+    return [sum(1 << b for b in bb[i * k:(i + 1) * k]) for i in range(n)]
+
+
+def port_core(q, T, topo):
+    c0 = T.cores[q]
+    for c in range(256):
+        if (topo.host(c) == topo.host(c0) and topo.chip(c) == topo.chip(c0) and c != c0 and topo.die(c) == topo.die(c0)
+                and all(topo.may_write(c, d) for d in T.cores)):
+            return c
+    return None
+
+
+def result_groups(q, T, topo):
+    c0, p = T.cores[q], port_core(q, T, topo)
+    direct = lambda r: topo.may_write(c0, T.cores[r])
+    out = []
+    for s, when, rs in ((c0, "a1", [r for r in (0, 1, 2) if r != q and direct(r)]),
+                        (c0, "a2", [r for r in (3,) if r != q and direct(r)]),
+                        (p, "p1", [r for r in (0, 1, 2) if r != q and not direct(r)]),
+                        (p, "p2", [7]),
+                        (p, "p3", [6] + [r for r in (3,) if r != q and not direct(r)]),
+                        (p, "p4", [4, 5])):
+        if rs:
+            m = 0xFFFF
+            for r in rs:
+                m &= topo.mask(s, T.cores[r])
+            out.append((s, when, rs, split(m, len(rs))))
+    return out
+
+
+def rank_program(g, core, T, topo):
+    ports = [port_core(q, T, topo) for q in range(N)]
+    rank = T.rank_of(core)
+    if rank is None and core not in ports:
+        return
+    isP = rank is None
+    q = ports.index(core) if isP else rank
+    c0, pc = T.cores[q], ports[q]
+    A = AluOpType
+    COPY = ActivationFunctionType.Copy
+    V, S, PE, SY = g.vector, g.scalar, g.tensor, g.sync
+    V_, S_, PE_, SY_, G_ = "V", "S", "P", "Y", "G"
+    eng = {V_: V, S_: S, PE_: PE, SY_: SY, G_: g}
+    evs, waited, cnt = [], {}, {"ls": 0}
+
+    def ev():
+        e = {"sem": T.sem["e%d" % len(evs)], "n": 0, "k": len(evs)}
+        evs.append(e)
+        return e
+
+    def ext(name, n):
+        return {"sem": T.sem[name], "n": n, "k": name}
+
+    def wait(qn, deps):
+        for e in deps:
+            key = (qn, e["k"])
+            if e["n"] and waited.get(key, 0) < e["n"]:
+                eng[qn].wait_ge(e["sem"], e["n"])
+                waited[key] = e["n"]
+
+    def do(qn, fn, args, deps, e=None, n=1, **kw):
+        wait(qn, deps)
+        if e is None:
+            e = ev()
+        fn(*args, **kw).then_inc(e["sem"], n)
+        e["n"] += n
+        return e
+
+    def dst(d):
+        rid, pid = topo.addr(d, core)
+        return DstId(rid=rid, pnc=pid)
+
+    def send(d, out, in_, sem, mask):
+        rid, pid = topo.addr(d, core)
+        g.remote_dma(out, in_, T.sem[sem], T.sem.lsem, pid, rid, mask)
+        cnt["ls"] += len(bits(mask))
+
+    def bcast(ds, ap, sem):
+        m = 0xFFFF
+        for d in ds:
+            m &= topo.mask(core, d)
+        g.remote_dma_fused([RemoteDMATransfer(dst_ids=[dst(d) for d in ds], dma_engine_mask=m, remote_sem=T.sem[sem],
+                                              srcs=[ap], dsts=[ap for d in ds])], local_sem=T.sem.lsem)
+        cnt["ls"] += len(bits(m))
+
+    mine = HB if isP else HA
+
+    def target(r, h):
+        return T.cores[r] if h in HA else ports[r]
+
+    if not isP:
+        eI = ev()
+        for k in range(4):
+            do(SY_, SY.dma_start, (T.IDXI[32 * k:32 * k + 16, :], T.idx[:]), [], eI, 16)
+            do(S_, S.dma_start, (T.IDXI[32 * k + 16:32 * k + 32, :], T.idx[:]), [], eI, 16)
+    eio = do(G_, g.iota, (T.IOI[:], [[1, 512]], 0, 0), [])
+    eDI = do(G_, g.iota, (T.DI[0:16, :], [[0, 8], [1, 16]], 0, -1), [], allow_small_or_imprecise_dtypes=True)
+    eKI = do(G_, g.iota, (T.KI[0:16, :], [[1, 96]], 0, -1), [], allow_small_or_imprecise_dtypes=True)
+    if not isP:
+        eEP = ev()
+        do(V_, V.memset, (T.EP[:, 0:20], 0), [], eEP)
+        do(V_, V.memset, (T.EP[:, 20:24], 32767), [], eEP)
+        eEnd = do(S_, S.dma_start, (T.EP[0:16, 4:20], T.end[:]), [eEP], None, 16)
+    m = ev()
+    for ap, v in ((T.C1[:, 0:1], -9e29), (T.C1[:, 1:2], -7.5e29), (T.win[:, 0:W0], -9e29), (T.win[:, W0 + R:], -9e29),
+                  (T.ACC[:], -9e29), (T.NB0[0:96, :], -9e29), (T.NB0[96:128, :], 1.4e28), (T.FW[:], 5000.0),
+                  (T.E8[0:16, :], 0.0), (T.IOT[96:128, :], 5000)):
+        do(V_, V.memset, (ap, v), [], m)
+    m2 = ev()
+    for o, i, s in ((T.NEG[:], T.C1[:, 0:1], 2.0), (T.POS[:], T.C1[:, 0:1], -2.0), (T.THR[:], T.C1[:, 1:2], 2.0),
+                    (T.win[:, 0:W0], T.win[:, 0:W0], 2.0), (T.win[:, W0 + R:], T.win[:, W0 + R:], 2.0),
+                    (T.ACC[:], T.ACC[:], 2.0), (T.NB[:], T.NB0[:], 4.0)):
+        do(V_, V.tensor_scalar, (o, i, s, None, A.mult), [m], m2)
+    eiot = do(V_, V.tensor_copy, (T.IOT[0:96, 0:512], T.IOI[0:96, :]), [eio, m])
+    eiot2 = ev()
+    for k in (1, 2, 3):
+        do(V_, V.tensor_scalar, (T.IOT[0:96, 512 * k:512 * k + 512], T.IOT[0:96, 0:512], 512.0 * k, None, A.add),
+           [eiot], eiot2)
+    own = T.IDX[:, 128 * q:128 * q + 128]
+    far = [target(r, q) for r in range(N) if r != q and not topo.may_write(c0, target(r, q))]
+    near = [target(r, q) for r in range(N) if r != q and topo.may_write(c0, target(r, q))]
+    nb = len(bits(topo.mask(c0, pc)))
+    tabd = []
+
+    def table(ks):
+        for k in ks:
+            tabd.append(do(SY_, SY.dma_start, (T.win[:, W0 + 512 * k:W0 + 512 * k + 512], T.tab[:, 512 * k:512 * k + 512]),
+                           [], None, 16))
+
+    if not isP:
+        eL = do(V_, V.tensor_copy, (own, T.IDXI[:]), [eI])
+        table(range(3))
+        wait(G_, [eL])
+        send(pc, own, own, "l%d" % q, topo.mask(core, pc))
+        bcast(near, own, "l%d" % q)
+        g.sem_inc(T.sem.go, 1)
+        wait(SY_, [ext("go", 1)])
+        table(range(3, 8))
+        endd = [eEnd, eEP]
+        wait(G_, endd)
+        send(pc, T.EP[:], T.EP[:], "endm", topo.mask(core, pc))
+        for k in range(4):
+            wait(G_, tabd[2 * k:2 * k + 2])
+            ap = T.win[:, W0 + 1024 * k:W0 + 1024 * k + 1024]
+            send(pc, ap, ap, "tab", topo.mask(core, pc))
+    else:
+        wait(G_, [ext("l%d" % q, nb)])
+        bcast(far, own, "l%d" % q)
+        endd, tabd = [ext("endm", nb)], [ext("tab", 4 * nb)]
+
+    def list_dep(h):
+        if not isP and h == q:
+            return eL
+        s = T.cores[h] if topo.may_write(T.cores[h], core) else ports[h]
+        return ext("l%d" % h, len(bits(topo.mask(s, core))))
+
+    cst = ev()
+    for ap, i, v in [(T.CREP, T.DI, 0.0), (T.CSH, T.DI, 1.0), (T.CWR, T.DI, -15.0)]:
+        do(V_, V.tensor_scalar, (ap[0:16, :], i[0:16, :], v, None, A.is_equal), [eDI], cst)
+    for k in range(6):
+        do(V_, V.tensor_scalar, (T.TK[0:16, 96 * k:96 * k + 96], T.KI[0:16, :], 16.0 * k, None, A.is_equal), [eKI], cst)
+    e8 = ev()
+    for h in mine:
+        do(V_, V.tensor_scalar, (T.E8[0:16, 4 + 8 * h + 2:4 + 8 * h + 8], T.EP[0:16, 2 * h + 2:2 * h + 8],
+                                 -2048.0 * h, 0.0, A.add, A.max), endd + [m], e8)
+    e8b = do(V_, V.tensor_scalar, (T.E8[0:16, :], T.E8[0:16, :], 2048.0, None, A.min), [e8, m])
+    pr = ev()
+    do(PE_, PE.matmul, (T.F1[:, 0:64], T.CREP[0:16, :], T.E8[0:16, 4:68], True, True), [e8b, cst], pr)
+    do(PE_, PE.matmul, (T.F1[:, 64:128], T.CSH[0:16, :], T.E8[0:16, 4:68], True, False), [], pr)
+    do(PE_, PE.matmul, (T.F1[:, 64:128], T.CWR[0:16, :], T.E8[0:16, 3:67], False, True), [], pr)
+    for k in range(6):
+        do(PE_, PE.matmul, (T.F1[0:96, 128:136], T.TK[0:16, 96 * k:96 * k + 96], T.E8[0:16, 6 + k:68:8], k == 0, k == 5),
+           [], pr)
+    ex = ev()
+    do(V_, V.tensor_copy, (T.FW[0:96, :], T.F1[0:96, 128:136]), [pr, m], ex)
+    do(V_, V.tensor_copy, (T.PVS[:], T.F1[:, 64:128]), [pr], ex)
+    ex2 = do(V_, V.tensor_tensor, (T.GT[:], T.F1[:, 0:64], T.PVS[:], A.is_gt), [ex])
+    ex3 = do(V_, V.tensor_tensor, (T.XO[:], T.F1[:, 0:64], T.GT[:], A.mult), [ex2])
+    eXU = do(V_, V.tensor_copy, (T.XU[:], T.XO[:]), [ex3])
+    eY = ev()
+    for k in range(2):
+        do(V_, V.tensor_copy, (T["Y%d" % k][:, 0:1], T.NEG[:]), [m2], eY)
+
+    eOH, eOFF, eF, scn, done = {}, {}, {}, {}, {}
+    nm = len(mine)
+
+    def onehot(n):
+        eOH[n] = do(V_, V.tensor_scalar, (T["OH%d" % n][:], T.IOT[:], T.FW[:, mine[n]:mine[n] + 1], None, A.is_equal),
+                    [ex, eiot, eiot2, m])
+
+    def offsets(n):
+        h = mine[n]
+        eOFF[n] = do(V_, V.tensor_scalar, (T.OFF[:, 128 * h:128 * h + 128], T.IDX[:, 128 * h:128 * h + 128],
+                                           float(W0 - R * q), float(W0 + R), A.add, A.min), [list_dep(h)])
+
+    def flags(n):
+        eF[n] = ev()
+        F = T["F%d" % (n % 2)]
+        for k in range(4):
+            do(PE_, PE.matmul, (F[:, 512 * k:512 * k + 512], T.NB[:], T["OH%d" % n][:, 512 * k:512 * k + 512], True, True),
+               [eOH[n], m2, ex3] + ([scn[n - 2]] if n >= 2 else []), eF[n])
+
+    for n in range(nm):
+        onehot(n)
+        if n < 2:
+            flags(n)
+        if n == 2:
+            offsets(0)
+    wd = T.win[:, 0:R + 8]
+    for n in range(nm):
+        h = mine[n]
+        X, Y, F = T["X%d" % (n % 3)], T["Y%d" % (n % 2)], T["F%d" % (n % 2)]
+        if n + 1 < nm:
+            offsets(n + 1)
+        o = 128 * h
+        dp = tabd + [eOFF[n], m2] + ([scn[n - 3]] if n >= 3 else [])
+        gv = do(V_, V.tensor_copy, (X[:, 0:VG], wd.indirect(T.OFF[:, o:o + VG // 16])), dp)
+        g1 = do(S_, S.activation, (X[:, VG:1024], wd.indirect(T.OFF[:, o + VG // 16:o + 64]), COPY), dp)
+        g2 = do(S_, S.activation, (X[:, 1024:2048], wd.indirect(T.OFF[:, o + 64:o + 128]), COPY), [])
+        s1 = do(V_, V.tensor_tensor_scan, (Y[:, 1:1025], F[:, 0:1024], X[:, 0:1024], T.NEG[:], A.min, A.max),
+                [gv, g1, eF[n], m2] + ([done[n - 2]] if n >= 2 else []))
+        scn[n] = do(V_, V.tensor_tensor_scan, (Y[:, 1025:2049], F[:, 1024:2048], X[:, 1024:2048], Y[:, 1024:1025],
+                                               A.min, A.max), [g2, s1])
+        if n + 2 < nm:
+            flags(n + 2)
+        lo, hi = (2 if h == 0 else 0), (4 if h == N - 1 else 6)
+        a = T.ACC[:, 32 * (h - 1) + 16 * lo:32 * (h - 1) + 16 * hi]
+        done[n] = do(V_, V.tensor_tensor, (a, Y[:].indirect(T.XU[:, 8 * h + 2 + lo:8 * h + 2 + hi]), a, A.max),
+                     [s1, scn[n], eXU, eY, m2] + ([done[n - 1]] if n else []))
+
+    groups = {w: (rs, ms) for s, w, rs, ms in result_groups(q, T, topo) if s == core}
+    acc = lambda r: T.ACC[:, B * r:B * r + B]
+    rl = lambda r: T.RL[:, B * r:B * r + B]
+
+    def results(w, buf, deps):
+        if w not in groups:
+            return
+        rs, ms = groups[w]
+        wait(G_, deps)
+        g.remote_dma_fused([RemoteDMATransfer(dst_ids=[dst(T.cores[r])], dma_engine_mask=mk, remote_sem=T.sem.res,
+                                              srcs=[buf(r)], dsts=[T.RES[:, B * q:B * q + B]])
+                            for r, mk in zip(rs, ms)], local_sem=T.sem.lsem)
+        cnt["ls"] += sum(len(bits(mk)) for mk in ms)
+
+    if not isP:
+        mk = topo.mask(core, pc)
+        wait(G_, [done[3]])
+        send(pc, T.RL[:, 0:96], T.ACC[:, 0:96], "rel1", mk)
+        results("a1", acc, [])
+        wait(G_, [done[4]])
+        send(pc, T.RL[:, 96:192], T.ACC[:, 96:192], "rel2", mk)
+        results("a2", acc, [])
+        fin = []
+        if q <= 3:
+            fin = [do(V_, V.tensor_copy, (T.RES[:, B * q:B * q + B], acc(q)), [done[4]])]
+        tot = 0
+        for k in range(N):
+            for s, w, rs, ms in result_groups(k, T, topo):
+                tot += sum(len(bits(x)) for r, x in zip(rs, ms) if r == q)
+        f1 = do(V_, V.tensor_tensor, (T.M1[:], T.RES[:, 0:128], T.RES[:, 128:256], A.max), fin + [ext("res", tot)])
+        f2 = do(V_, V.tensor_tensor, (T.M2[:], T.M1[:, 0:64], T.M1[:, 64:128], A.max), [f1])
+        f3 = do(V_, V.tensor_tensor, (T.M3[:], T.M2[:, 0:32], T.M2[:, 32:64], A.max), [f2])
+        f4 = do(V_, V.tensor_scalar, (T.M4[:], T.M3[:], T.THR[:], T.POS[:], A.is_le, A.mult), [f3, m2])
+        f5 = do(V_, V.tensor_tensor, (T.YO[:], T.M3[:], T.M4[:], A.add), [f4])
+        do(SY_, SY.dma_start, (T.y[:], T.YO[:]), [f5], None, 16)
+    else:
+        mg = do(V_, V.tensor_tensor, (T.ACC[:, 128:192], T.ACC[:, 128:192], T.RL[:, 128:192], A.max),
+                [done[2], ext("rel2", nb)])
+        wait(G_, [ext("rel1", nb)])
+        results("p1", rl, [])
+        results("p2", acc, [done[1]])
+        results("p3", lambda r: acc(r) if r >= 4 else rl(r), [done[2], ext("rel2", nb)])
+        results("p4", acc, [mg])
+    g.wait_ge(T.sem.lsem, cnt["ls"])
+    for e in evs:
+        if e["n"] and not any(waited.get((qn, e["k"]), 0) >= e["n"] for qn in eng):
+            g.wait_ge(e["sem"], e["n"])

@@ -1,23 +1,24 @@
 from concourse.bass import DstId, RemoteDMATransfer
 from concourse.mybir import AluOpType, ActivationFunctionType
 
-N, R, E, B = 8, 4096, 2048, 32
-HA = [0, 1, 2, 3, 4]
-HB = [7, 6, 5]
-W0 = 4
-VG = 256
-NEV = 132
+N, R, E, B, CAP = 8, 4096, 2048, 32, 512
+MID = R // 2
+NEV = 124
+COLS = ["AC", "FC", "J0", "WF", "IV", "KV", "T1", "T2", "ECF", "CW", "NEG", "POS", "THR", "CA", "CB"]
+SLOT = ["GE", "VV", "VW", "VO", "KR", "NJ", "MK", "RK", "PV", "GT", "XO", "SF", "SG"]
 
-SCRATCH = {"F0": ("psum", [128, E], "float32"), "F1": ("psum", [128, E], "float32")}
-for _t, _l in (("float32", dict(win=R + 8, E8=72, DI=128, KI=96, CREP=128, CSH=128, CWR=128, TK=576, FW=8, PVS=64, GT=64,
-                                XO=64, ACC=256, RL=192, RES=256, M1=128, M2=64, M3=32, M4=32, YO=32, C1=2, NEG=1, POS=1,
-                                THR=1, X0=E, X1=E, X2=E, Y0=E + 1, Y1=E + 1)),
-               ("int32", dict(IDXI=128, IOI=512, EP=24)),
-               ("uint16", dict(IDX=1024, OFF=1024, IOT=E, XU=64)),
-               ("bfloat16", dict(NB0=128, NB=128, OH0=E, OH1=E, OH2=E, OH3=E, OH4=E))):
+SCRATCH = {"p%s" % k: ("psum", [128, 512], "float32") for k in "ABCDEF"}
+for _t, _l in (("float32", dict(win=R + 1, AF=128, FF=128, MI=128, D2=128, ID=128, DG=96, ONF=128, CREP=128, CSH=128, CWR=128,
+                                TA=128, TB2=128, S=16, Q=16 * len(SLOT), ACC=256, RL=256, RES=256, M=288,
+                                X0=CAP, X1=CAP, X2=CAP, Y0=CAP + 1, Y1=CAP + 1)),
+               ("int32", dict(MSG=20, RLY=20, IOI=CAP, I1=4, I2=80)),
+               ("uint16", dict(IM=128, IC=32, IOT=CAP, OUTA=32, OUTC=8, OF=40 * N)),
+               ("float16", dict(LH=128 * 16, RH=32 * 16)),
+               ("bfloat16", dict(NB0=128, NB=128, OHF=CAP, FLM=CAP, FL=CAP * N, A1=128, A2=128, A32=128, O=16, INC=16, TB=16,
+                                 ON=96, ONB=16, SG=96 * 16))):
     for _n, _w in _l.items():
         SCRATCH[_n] = ("sbuf", [128, _w], _t)
-SEMAPHORES = (["l%d" % h for h in range(N)] + ["res", "tab", "endm", "rel1", "rel2", "lsem", "go"]
+SEMAPHORES = (["of%d" % h for h in range(N)] + ["fl%d" % h for h in range(N)] + ["res", "lm", "lr", "rel", "lsem", "go"]
               + ["e%d" % k for k in range(NEV)])
 
 
@@ -33,47 +34,47 @@ def split(mask, n):
     return [sum(1 << b for b in bb[i * k:(i + 1) * k]) for i in range(n)]
 
 
-def port_core(q, T, topo):
+def common(core, ds, topo):
+    m = 0xFFFF
+    for d in ds:
+        m &= topo.mask(core, d)
+    return m
+
+
+def chip_plan(q, T, topo):
     c0 = T.cores[q]
-    for c in range(256):
-        if (topo.host(c) == topo.host(c0) and topo.chip(c) == topo.chip(c0) and c != c0 and topo.die(c) == topo.die(c0)
-                and all(topo.may_write(c, d) for d in T.cores)):
-            return c
-    return None
-
-
-def result_groups(q, T, topo):
-    c0, p = T.cores[q], port_core(q, T, topo)
-    direct = lambda r: topo.may_write(c0, T.cores[r])
-    out = []
-    for s, when, rs in ((c0, "a1", [r for r in (0, 1, 2) if r != q and direct(r)]),
-                        (c0, "a2", [r for r in (3,) if r != q and direct(r)]),
-                        (p, "p1", [r for r in (0, 1, 2) if r != q and not direct(r)]),
-                        (p, "p2", [7]),
-                        (p, "p3", [6] + [r for r in (3,) if r != q and not direct(r)]),
-                        (p, "p4", [4, 5])):
-        if rs:
-            m = 0xFFFF
-            for r in rs:
-                m &= topo.mask(s, T.cores[r])
-            out.append((s, when, rs, split(m, len(rs))))
-    return out
+    cs = [c for c in range(256) if topo.host(c) == topo.host(c0) and topo.chip(c) == topo.chip(c0) and c != c0]
+    mate = [c for c in cs if topo.die(c) == topo.die(c0)]
+    p = [c for c in mate if all(topo.may_write(c, d) for d in T.cores)][0]
+    far = [h for h in range(N) if not topo.may_write(T.cores[h], c0) and h != q]
+    nea = [h for h in range(N) if topo.may_write(T.cores[h], c0) and h != q]
+    order = [p] + [c for c in mate if c != p] + [c for c in cs if c not in mate]
+    return p, dict([(q, c0)] + list(zip(far + nea, order)))
 
 
 def rank_program(g, core, T, topo):
-    ports = [port_core(q, T, topo) for q in range(N)]
-    rank = T.rank_of(core)
-    if rank is None and core not in ports:
+    plans = [chip_plan(r, T, topo) for r in range(N)]
+    ports = [p[0] for p in plans]
+    role = [(r, h) for r in range(N) for h in range(N) if plans[r][1][h] == core]
+    if not role:
         return
-    isP = rank is None
-    q = ports.index(core) if isP else rank
+    q, h = role[0]
     c0, pc = T.cores[q], ports[q]
+    is0, isP = core == c0, core == pc
+    near = lambda r, s: topo.may_write(T.cores[r], T.cores[s])
     A = AluOpType
-    COPY = ActivationFunctionType.Copy
+    COPY, SIGN = ActivationFunctionType.Copy, ActivationFunctionType.Sign
     V, S, PE, SY = g.vector, g.scalar, g.tensor, g.sync
-    V_, S_, PE_, SY_, G_ = "V", "S", "P", "Y", "G"
-    eng = {V_: V, S_: S, PE_: PE, SY_: SY, G_: g}
+    eng = {"V": V, "S": S, "P": PE, "Y": SY, "G": g}
     evs, waited, cnt = [], {}, {"ls": 0}
+
+    def c_(name, P=128):
+        k = COLS.index(name)
+        return T.S[0:P, k:k + 1]
+
+    def q_(name, a=0, b=16, P=128):
+        k = 16 * SLOT.index(name)
+        return T.Q[0:P, k + a:k + b]
 
     def ev():
         e = {"sem": T.sem["e%d" % len(evs)], "n": 0, "k": len(evs)}
@@ -98,6 +99,21 @@ def rank_program(g, core, T, topo):
         e["n"] += n
         return e
 
+    def ts(out, i, s1, op, deps, e=None, s2=None, op2=None):
+        return do("V", V.tensor_scalar, (out, i, s1, s2, op) + ((op2,) if op2 is not None else ()), deps, e)
+
+    def tt(out, a, b, op, deps, e=None):
+        return do("V", V.tensor_tensor, (out, a, b, op), deps, e)
+
+    def cp(out, i, deps, e=None):
+        return do("V", V.tensor_copy, (out, i), deps, e)
+
+    def mm(out, l, r, a, b, deps, e=None):
+        return do("P", PE.matmul, (out, l, r, a, b), deps, e)
+
+    def iota(ap, pat, base, cm, e):
+        do("G", g.iota, (ap, pat, base, cm), [], e, allow_small_or_imprecise_dtypes=True)
+
     def dst(d):
         rid, pid = topo.addr(d, core)
         return DstId(rid=rid, pnc=pid)
@@ -107,203 +123,216 @@ def rank_program(g, core, T, topo):
         g.remote_dma(out, in_, T.sem[sem], T.sem.lsem, pid, rid, mask)
         cnt["ls"] += len(bits(mask))
 
-    def bcast(ds, ap, sem):
-        m = 0xFFFF
-        for d in ds:
-            m &= topo.mask(core, d)
-        g.remote_dma_fused([RemoteDMATransfer(dst_ids=[dst(d) for d in ds], dma_engine_mask=m, remote_sem=T.sem[sem],
-                                              srcs=[ap], dsts=[ap for d in ds])], local_sem=T.sem.lsem)
-        cnt["ls"] += len(bits(m))
+    def fused(trs):
+        g.remote_dma_fused([RemoteDMATransfer(dst_ids=[dst(d) for d in ds], dma_engine_mask=mk, remote_sem=T.sem[sem],
+                                              srcs=[src], dsts=[out for d in ds]) for ds, src, out, sem, mk in trs],
+                           local_sem=T.sem.lsem)
+        cnt["ls"] += sum(len(bits(x[4])) for x in trs)
 
-    mine = HB if isP else HA
+    tn = lambda r: [plans[s][1][r] for s in range(N) if s != r and near(r, s)]
+    tf = lambda r: [plans[s][1][r] for s in range(N) if s != r and not near(r, s)]
+    mrel = lambda r: topo.mask(T.cores[r], ports[r]) & common(T.cores[r], tn(r), topo)
+    KC, k0 = (4 if h in (0, N - 1) else 6), max(0, 2 * h - 2)
+    W = 16 * KC
 
-    def target(r, h):
-        return T.cores[r] if h in HA else ports[r]
-
-    if not isP:
-        eI = ev()
-        for k in range(4):
-            do(SY_, SY.dma_start, (T.IDXI[32 * k:32 * k + 16, :], T.idx[:]), [], eI, 16)
-            do(S_, S.dma_start, (T.IDXI[32 * k + 16:32 * k + 32, :], T.idx[:]), [], eI, 16)
-    eio = do(G_, g.iota, (T.IOI[:], [[1, 512]], 0, 0), [])
-    eDI = do(G_, g.iota, (T.DI[0:16, :], [[0, 8], [1, 16]], 0, -1), [], allow_small_or_imprecise_dtypes=True)
-    eKI = do(G_, g.iota, (T.KI[0:16, :], [[1, 96]], 0, -1), [], allow_small_or_imprecise_dtypes=True)
-    if not isP:
-        eEP = ev()
-        do(V_, V.memset, (T.EP[:, 0:20], 0), [], eEP)
-        do(V_, V.memset, (T.EP[:, 20:24], 32767), [], eEP)
-        eEnd = do(S_, S.dma_start, (T.EP[0:16, 4:20], T.end[:]), [eEP], None, 16)
-    m = ev()
-    for ap, v in ((T.C1[:, 0:1], -9e29), (T.C1[:, 1:2], -7.5e29), (T.win[:, 0:W0], -9e29), (T.win[:, W0 + R:], -9e29),
-                  (T.ACC[:], -9e29), (T.NB0[0:96, :], -9e29), (T.NB0[96:128, :], 1.4e28), (T.FW[:], 5000.0),
-                  (T.E8[0:16, :], 0.0), (T.IOT[96:128, :], 5000)):
-        do(V_, V.memset, (ap, v), [], m)
-    m2 = ev()
-    for o, i, s in ((T.NEG[:], T.C1[:, 0:1], 2.0), (T.POS[:], T.C1[:, 0:1], -2.0), (T.THR[:], T.C1[:, 1:2], 2.0),
-                    (T.win[:, 0:W0], T.win[:, 0:W0], 2.0), (T.win[:, W0 + R:], T.win[:, W0 + R:], 2.0),
-                    (T.ACC[:], T.ACC[:], 2.0), (T.NB[:], T.NB0[:], 4.0)):
-        do(V_, V.tensor_scalar, (o, i, s, None, A.mult), [m], m2)
-    eiot = do(V_, V.tensor_copy, (T.IOT[0:96, 0:512], T.IOI[0:96, :]), [eio, m])
-    eiot2 = ev()
-    for k in (1, 2, 3):
-        do(V_, V.tensor_scalar, (T.IOT[0:96, 512 * k:512 * k + 512], T.IOT[0:96, 0:512], 512.0 * k, None, A.add),
-           [eiot], eiot2)
-    own = T.IDX[:, 128 * q:128 * q + 128]
-    far = [target(r, q) for r in range(N) if r != q and not topo.may_write(c0, target(r, q))]
-    near = [target(r, q) for r in range(N) if r != q and topo.may_write(c0, target(r, q))]
-    nb = len(bits(topo.mask(c0, pc)))
-    tabd = []
-
-    def table(ks):
-        for k in ks:
-            tabd.append(do(SY_, SY.dma_start, (T.win[:, W0 + 512 * k:W0 + 512 * k + 512], T.tab[:, 512 * k:512 * k + 512]),
-                           [], None, 16))
-
-    if not isP:
-        eL = do(V_, V.tensor_copy, (own, T.IDXI[:]), [eI])
-        table(range(3))
-        wait(G_, [eL])
-        send(pc, own, own, "l%d" % q, topo.mask(core, pc))
-        bcast(near, own, "l%d" % q)
-        g.sem_inc(T.sem.go, 1)
-        wait(SY_, [ext("go", 1)])
-        table(range(3, 8))
-        endd = [eEnd, eEP]
-        wait(G_, endd)
-        send(pc, T.EP[:], T.EP[:], "endm", topo.mask(core, pc))
-        for k in range(4):
-            wait(G_, tabd[2 * k:2 * k + 2])
-            ap = T.win[:, W0 + 1024 * k:W0 + 1024 * k + 1024]
-            send(pc, ap, ap, "tab", topo.mask(core, pc))
+    zc = ev()
+    if is0:
+        eI = do("Y", SY.dma_start, (T.MSG[:, 0:16], T.idx[:]), [], None, 16)
+        do("V", V.memset, (T.MSG[:, 16:20], 0), [], zc)
+        eE = do("S", S.dma_start, (T.MSG[0:W, 16:17], T.end[:, k0:k0 + KC]), [zc], None, 16)
+        msgd = [eI, eE, zc]
     else:
-        wait(G_, [ext("l%d" % q, nb)])
-        bcast(far, own, "l%d" % q)
-        endd, tabd = [ext("endm", nb)], [ext("tab", 4 * nb)]
+        s = T.cores[h] if near(h, q) else ports[h]
+        msgd = [ext("lm", len(bits(common(s, tn(h) if near(h, q) else tf(h), topo))))]
+    c1 = ev()
+    iota(T.I1[:, 0:1], [[0, 1]], 0, 1, c1)
+    iota(T.AF[:], [[0, 16], [1, 8]], 0, 0, c1)
+    iota(T.FF[:], [[1, 16], [0, 8]], 0, 0, c1)
+    iota(T.MI[:], [[0, 8], [1, 16]], 0, 0, c1)
+    iota(q_("KR"), [[16, 16]], 0, 0, c1)
+    if is0:
+        wait("G", msgd)
+        send(pc, T.RLY[:], T.MSG[:], "lr", mrel(q))
+        fused([(tn(q), T.MSG[:], T.MSG[:], "lm", common(core, tn(q), topo))])
+        g.sem_inc(T.sem.go, 1)
+    c2 = ev()
+    iota(T.ID[0:96, 0:96], [[1, 96]], 0, -1, c2)
+    iota(T.D2[0:W, :], [[0, 8], [KC, 16]], 0, -1, c2)
+    iota(T.IOI[:], [[1, CAP]], 0, 0, c2)
+    iota(c_("WF"), [[0, 1]], 0, 1, c2)
+    if isP:
+        wait("G", [ext("lr", len(bits(mrel(q))))])
+        fused([(tf(q), T.RLY[:], T.MSG[:], "lm", common(core, tf(q), topo))])
 
-    def list_dep(h):
-        if not isP and h == q:
-            return eL
-        s = T.cores[h] if topo.may_write(T.cores[h], core) else ports[h]
-        return ext("l%d" % h, len(bits(topo.mask(s, core))))
-
+    m = ev()
+    for ap, v in ((c_("CA"), -9e29), (c_("CB"), -7.5e29), (T.NB0[0:96, :], -9e29), (T.NB0[96:128, :], 1.4e28),
+                  (c_("CW"), 5000.0), (T.IOT[96:128, :], 5000), (q_("RK"), 0.0), (T.OUTC[:], 0),
+                  (T.ONB[:], 1.0), (T.ON[:], 1.0), (T.ONF[:], 1.0)) + (((T.ACC[:], -9e29),) if is0 else ()):
+        do("V", V.memset, (ap, v), [], m)
+    m2 = ev()
+    for o, i, s in ((c_("NEG"), c_("CA"), 2.0), (c_("POS"), c_("CA"), -2.0), (c_("THR"), c_("CB"), 2.0),
+                    (T.NB[:], T.NB0[:], 4.0), (T.win[:, MID:MID + 1], c_("CA"), 2.0)) + (
+                        ((T.ACC[:], T.ACC[:], 2.0),) if is0 else ()):
+        ts(o, i, s, A.mult, [m], m2)
+    a = ev()
+    ts(T.I1[:, 1:2], T.I1[:, 0:1], 7, A.bitwise_and, [c1], a)
+    ts(T.I1[:, 2:3], T.I1[:, 0:1], 3, A.arith_shift_right, [c1], a)
+    b = ev()
+    cp(c_("AC"), T.I1[:, 1:2], [a], b)
+    cp(c_("FC"), T.I1[:, 2:3], [a], b)
     cst = ev()
-    for ap, i, v in [(T.CREP, T.DI, 0.0), (T.CSH, T.DI, 1.0), (T.CWR, T.DI, -15.0)]:
-        do(V_, V.tensor_scalar, (ap[0:16, :], i[0:16, :], v, None, A.is_equal), [eDI], cst)
-    for k in range(6):
-        do(V_, V.tensor_scalar, (T.TK[0:16, 96 * k:96 * k + 96], T.KI[0:16, :], 16.0 * k, None, A.is_equal), [eKI], cst)
-    e8 = ev()
-    for h in mine:
-        do(V_, V.tensor_scalar, (T.E8[0:16, 4 + 8 * h + 2:4 + 8 * h + 8], T.EP[0:16, 2 * h + 2:2 * h + 8],
-                                 -2048.0 * h, 0.0, A.add, A.max), endd + [m], e8)
-    e8b = do(V_, V.tensor_scalar, (T.E8[0:16, :], T.E8[0:16, :], 2048.0, None, A.min), [e8, m])
-    pr = ev()
-    do(PE_, PE.matmul, (T.F1[:, 0:64], T.CREP[0:16, :], T.E8[0:16, 4:68], True, True), [e8b, cst], pr)
-    do(PE_, PE.matmul, (T.F1[:, 64:128], T.CSH[0:16, :], T.E8[0:16, 4:68], True, False), [], pr)
-    do(PE_, PE.matmul, (T.F1[:, 64:128], T.CWR[0:16, :], T.E8[0:16, 3:67], False, True), [], pr)
-    for k in range(6):
-        do(PE_, PE.matmul, (T.F1[0:96, 128:136], T.TK[0:16, 96 * k:96 * k + 96], T.E8[0:16, 6 + k:68:8], k == 0, k == 5),
-           [], pr)
-    ex = ev()
-    do(V_, V.tensor_copy, (T.FW[0:96, :], T.F1[0:96, 128:136]), [pr, m], ex)
-    do(V_, V.tensor_copy, (T.PVS[:], T.F1[:, 64:128]), [pr], ex)
-    ex2 = do(V_, V.tensor_tensor, (T.GT[:], T.F1[:, 0:64], T.PVS[:], A.is_gt), [ex])
-    ex3 = do(V_, V.tensor_tensor, (T.XO[:], T.F1[:, 0:64], T.GT[:], A.mult), [ex2])
-    eXU = do(V_, V.tensor_copy, (T.XU[:], T.XO[:]), [ex3])
-    eY = ev()
-    for k in range(2):
-        do(V_, V.tensor_copy, (T["Y%d" % k][:, 0:1], T.NEG[:]), [m2], eY)
+    cp(T.IM[:], T.MI[:], [c1], cst)
+    cp(T.IC[:, 0:16], T.MI[:, 0:16], [c1], cst)
+    ts(T.IC[:, 16:32], T.MI[:, 0:16], 16.0, A.add, [c1], cst)
+    ts(T.A1[:], T.AF[:], c_("AC"), A.is_gt, [b], cst)
+    eA2 = ts(T.A2[:], T.AF[:], c_("AC"), A.is_equal, [b])
+    e = ts(T.TA[:], T.FF[:], c_("FC"), A.is_gt, [b])
+    e = tt(T.TB2[:], T.TA[:], T.A2[:], A.mult, [e, eA2])
+    tt(T.A32[:], T.TB2[:], T.A2[:], A.subtract, [e], cst)
+    e = ts(c_("T1"), c_("AC"), 256.0, A.mult, [b], None, 0.5, A.add)
+    e = tt(c_("J0"), c_("T1"), c_("FC"), A.add, [e])
+    ts(q_("NJ"), q_("KR"), c_("J0"), A.add, [e], cst, -1.0, A.mult)
+    if is0:
+        tabd = [do("Y", SY.dma_start, (T.win[:, 0:512], T.tab[:, 0:512]), [], None, 16)]
+        wait("Y", [ext("go", 1), m2])
+        tabd.append(do("Y", SY.dma_start, (T.win[:, 512:MID], T.tab[:, 512:MID]), [], None, 16))
+        tabd.append(do("Y", SY.dma_start, (T.win[:, MID + 1:], T.tab[:, MID:]), [], None, 16))
 
-    eOH, eOFF, eF, scn, done = {}, {}, {}, {}, {}
-    nm = len(mine)
+    def late_constants():
+        k = ev()
+        ts(T.ID[0:96, 0:96], T.ID[0:96, 0:96], 0.0, A.is_equal, [c2], k)
+        cp(T.IOT[0:96, :], T.IOI[0:96, :], [c2, m], k)
+        x = ev()
+        ts(T.CREP[0:W, :], T.D2[0:W, :], -float(KC), A.is_gt, [c2], x)
+        ts(T.CSH[0:W, :], T.D2[0:W, :], 0.0, A.is_gt, [c2], x)
+        ts(T.TA[0:W, :], T.D2[0:W, :], 0.0, A.is_le, [c2, cst], x)
+        ts(T.TB2[0:W, :], T.D2[0:W, :], float(KC), A.is_le, [c2, cst], x)
+        ts(T.CWR[0:W, :], T.D2[0:W, :], -15.0 * KC, A.is_le, [c2], k)
+        tt(T.CREP[0:W, :], T.CREP[0:W, :], T.TA[0:W, :], A.mult, [x], k)
+        tt(T.CSH[0:W, :], T.CSH[0:W, :], T.TB2[0:W, :], A.mult, [x], k)
+        e = ts(c_("T2"), c_("WF"), 1.0 / KC, A.mult, [c2], None, -0.5 + 0.5 / KC, A.add)
+        e = cp(T.I1[:, 3:4], c_("T2"), [e])
+        e = cp(c_("IV"), T.I1[:, 3:4], [e])
+        e = ts(c_("KV"), c_("IV"), -float(KC), A.mult, [e], None, c_("WF"), A.add)
+        ts(q_("MK", 0, 8), T.IC[:, 0:8], c_("KV"), A.is_equal, [e, cst], k)
+        return k
 
-    def onehot(n):
-        eOH[n] = do(V_, V.tensor_scalar, (T["OH%d" % n][:], T.IOT[:], T.FW[:, mine[n]:mine[n] + 1], None, A.is_equal),
-                    [ex, eiot, eiot2, m])
+    k2 = None if is0 else late_constants()
 
-    def offsets(n):
-        h = mine[n]
-        eOFF[n] = do(V_, V.tensor_scalar, (T.OFF[:, 128 * h:128 * h + 128], T.IDX[:, 128 * h:128 * h + 128],
-                                           float(W0 - R * q), float(W0 + R), A.add, A.min), [list_dep(h)])
+    OW, CL, SI, SJ = T.I2[:, 0:16], T.I2[:, 16:32], T.I2[:, 32:48], T.I2[:, 48:80]
+    e = ts(OW, T.MSG[:, 0:16], 12, A.arith_shift_right, msgd)
+    eO = ts(T.O[:], OW, float(q), A.is_equal, [e])
+    eIn = do("V", V.tensor_tensor_scan, (T.INC[:], T.ONB[:], T.O[:], 0.0, A.mult, A.add), [eO, m])
+    eTB = ts(T.TB[:], T.ONB[:], T.INC[:, 15:16], A.mult, [eIn])
+    eX = ev()
+    mm(T.pA[:, 0:16], T.A2[:], T.INC[:], True, False, [eIn, cst, eA2], eX)
+    mm(T.pA[:, 0:16], T.A32[:], T.O[:], False, False, [eO], eX)
+    mm(T.pA[:, 0:16], T.A1[:], T.TB[:], False, True, [eTB], eX)
+    if k2 is None:
+        k2 = late_constants()
+    e = ts(c_("ECF", W), T.MSG[0:W, 16:17], -float(E * h), A.add, [])
+    eD = ts(T.DG[0:W, 0:W], T.ID[0:W, 0:W], c_("ECF", W), A.mult, [e, k2])
+    eEF = mm(T.pF[:, 0:W], T.ONF[0:W, :], T.DG[0:W, 0:W], True, True, [eD, m])
+    eS = []
+    for k in range(0, 16, 2):
+        x = ev()
+        for t in (k, k + 1):
+            do("S", S.activation, (T.SG[:, 96 * t:96 * t + W], T.pF[:, 0:W], SIGN, q_("NJ", t, t + 1)), [eEF, cst], x)
+        eS.append(x)
+    e = cp(SI, T.pA[:, 0:16], [eX])
+    x = ev()
+    ts(T.I2[:, 48:64], SI, 15, A.bitwise_and, [e], x)
+    ts(T.I2[:, 64:80], SI, 4, A.arith_shift_right, [e], x)
+    eSF = cp(q_("SF", 0, 32), SJ, [x])
+    eC = ts(CL, T.MSG[:, 0:16], R - 1, A.bitwise_and, [])
+    e = ts(q_("GE"), CL, float(MID), A.is_ge, [eC])
+    e = tt(q_("VV"), CL, q_("GE"), A.add, [e])
+    e = ts(q_("VW"), q_("VV"), -float(MID), A.add, [e])
+    eVO = tt(q_("VO"), q_("VW"), T.O[:], A.mult, [e])
+    eP, eCn = ev(), ev()
+    mm(T.pC[0:W, 0:1], T.ON[:, 0:W], T.INC[:, 15:16], True, False, [m], eCn)
+    for k in range(0, 16, 2):
+        x = ev()
+        for t in (k, k + 1):
+            ts(T.LH[:, 128 * t:128 * t + 128], T.IM[:], q_("SF", t, t + 1), A.is_equal, [eSF, cst], x)
+            ts(T.RH[:, 32 * t:32 * t + 32], T.IC[:], q_("SF", 16 + t, 17 + t), A.is_equal, [eVO], x, q_("VO", t, t + 1), A.mult)
+        for t in (k, k + 1):
+            mm(T.pB[:, 0:32], T.LH[:, 128 * t:128 * t + 128], T.RH[:, 32 * t:32 * t + 32], t == 0, t == 15, [x], eP)
+            mm(T.pC[0:W, 0:1], T.SG[:, 96 * t:96 * t + W], T.O[:, t:t + 1], False, t == 15, [eS[k // 2]], eCn)
+    eA = ts(T.OUTA[:], T.pB[:, 0:32], float(MID), A.add, [eP])
+    mrep = topo.mask(core, c0)
+    nrep = lambda c: len(bits(topo.mask(c, c0)))
+    if not is0:
+        wait("G", [eA])
+        send(c0, T.OF[:, 40 * h:40 * h + 32], T.OUTA[:], "of%d" % h, mrep)
+    e = ts(c_("CW", W), T.pC[0:W, 0:1], 0.5, A.mult, [eCn, m])
+    eOH = ts(T.OHF[:], T.IOT[:], c_("CW"), A.is_equal, [e, k2, m])
+    eRK = ts(q_("RK", 1, 1 + KC, W), q_("MK", 0, KC, W), c_("CW", W), A.mult, [e, k2, m])
+    eFl = mm(T.pE[:], T.NB[:], T.OHF[:], True, True, [eOH, m2])
+    eR = ev()
+    rk, rk1 = q_("RK", 1, 1 + KC, W), q_("RK", 0, KC, W)
+    mm(T.pD[:, 0:KC], T.CREP[0:W, :], rk, True, True, [eRK], eR)
+    mm(T.pD[:, 8:8 + KC], T.CSH[0:W, :], rk, True, False, [], eR)
+    mm(T.pD[:, 8:8 + KC], T.CWR[0:W, :], rk1, False, True, [], eR)
+    eFM = do("S", S.activation, (T.FLM[:], T.pE[:], COPY), [eFl])
+    e = cp(q_("PV", 0, KC), T.pD[:, 8:8 + KC], [eR])
+    e = tt(q_("GT", 0, KC), T.pD[:, 0:KC], q_("PV", 0, KC), A.is_gt, [e])
+    e = tt(q_("XO", 0, KC), T.pD[:, 0:KC], q_("GT", 0, KC), A.mult, [e])
+    eC2 = cp(T.OUTC[:, 0:KC], q_("XO", 0, KC), [e, m])
+    if not is0:
+        wait("G", [eFM])
+        send(c0, T.FL[:, CAP * h:CAP * h + CAP], T.FLM[:], "fl%d" % h, mrep)
+        wait("G", [eC2])
+        send(c0, T.OF[:, 40 * h + 32:40 * h + 40], T.OUTC[:], "fl%d" % h, mrep)
 
-    def flags(n):
-        eF[n] = ev()
-        F = T["F%d" % (n % 2)]
-        for k in range(4):
-            do(PE_, PE.matmul, (F[:, 512 * k:512 * k + 512], T.NB[:], T["OH%d" % n][:, 512 * k:512 * k + 512], True, True),
-               [eOH[n], m2, ex3] + ([scn[n - 2]] if n >= 2 else []), eF[n])
+    col = lambda r: slice(B * r, B * r + B)
+    if is0:
+        eY = ev()
+        for k in range(2):
+            cp(T["Y%d" % k][:, 0:1], c_("NEG"), [m2], eY)
+        order = [q] + [r for r in range(N) if r != q and near(r, q)] + [r for r in range(N) if r != q and not near(r, q)]
+        scn, done = {}, {}
+        for n, r in enumerate(order):
+            X, Y = T["X%d" % (n % 3)], T["Y%d" % (n % 2)]
+            kc, kk = (4 if r in (0, N - 1) else 6), max(0, 2 * r - 2)
+            if r == q:
+                off, fl, xo, d1, d2 = T.OUTA[:], T.FLM[:], T.OUTC[:, 0:kc], [eA], [eFM, eC2]
+            else:
+                off, fl = T.OF[:, 40 * r:40 * r + 32], T.FL[:, CAP * r:CAP * r + CAP]
+                xo = T.OF[:, 40 * r + 32:40 * r + 32 + kc]
+                d1, d2 = [ext("of%d" % r, nrep(plans[q][1][r]))], [ext("fl%d" % r, 2 * nrep(plans[q][1][r]))]
+            ga = do("S", S.activation, (X[:], T.win[:].indirect(off), COPY), tabd + [m2] + d1 + ([scn[n - 3]] if n > 2 else []))
+            scn[n] = do("V", V.tensor_tensor_scan, (Y[:, 1:], fl, X[:], c_("NEG"), A.min, A.max),
+                        [ga, m2, eY] + d2 + ([done[n - 2]] if n > 1 else []))
+            acc = T.ACC[:, 16 * kk:16 * kk + 16 * kc]
+            done[n] = tt(acc, Y[:].indirect(xo), acc, A.max, [scn[n]] + ([done[n - 1]] if n else []))
 
-    for n in range(nm):
-        onehot(n)
-        if n < 2:
-            flags(n)
-        if n == 2:
-            offsets(0)
-    wd = T.win[:, 0:R + 8]
-    for n in range(nm):
-        h = mine[n]
-        X, Y, F = T["X%d" % (n % 3)], T["Y%d" % (n % 2)], T["F%d" % (n % 2)]
-        if n + 1 < nm:
-            offsets(n + 1)
-        o = 128 * h
-        dp = tabd + [eOFF[n], m2] + ([scn[n - 3]] if n >= 3 else [])
-        gv = do(V_, V.tensor_copy, (X[:, 0:VG], wd.indirect(T.OFF[:, o:o + VG // 16])), dp)
-        g1 = do(S_, S.activation, (X[:, VG:1024], wd.indirect(T.OFF[:, o + VG // 16:o + 64]), COPY), dp)
-        g2 = do(S_, S.activation, (X[:, 1024:2048], wd.indirect(T.OFF[:, o + 64:o + 128]), COPY), [])
-        s1 = do(V_, V.tensor_tensor_scan, (Y[:, 1:1025], F[:, 0:1024], X[:, 0:1024], T.NEG[:], A.min, A.max),
-                [gv, g1, eF[n], m2] + ([done[n - 2]] if n >= 2 else []))
-        scn[n] = do(V_, V.tensor_tensor_scan, (Y[:, 1025:2049], F[:, 1024:2048], X[:, 1024:2048], Y[:, 1024:1025],
-                                               A.min, A.max), [g2, s1])
-        if n + 2 < nm:
-            flags(n + 2)
-        lo, hi = (2 if h == 0 else 0), (4 if h == N - 1 else 6)
-        a = T.ACC[:, 32 * (h - 1) + 16 * lo:32 * (h - 1) + 16 * hi]
-        done[n] = do(V_, V.tensor_tensor, (a, Y[:].indirect(T.XU[:, 8 * h + 2 + lo:8 * h + 2 + hi]), a, A.max),
-                     [s1, scn[n], eXU, eY, m2] + ([done[n - 1]] if n else []))
-
-    groups = {w: (rs, ms) for s, w, rs, ms in result_groups(q, T, topo) if s == core}
-    acc = lambda r: T.ACC[:, B * r:B * r + B]
-    rl = lambda r: T.RL[:, B * r:B * r + B]
-
-    def results(w, buf, deps):
-        if w not in groups:
-            return
-        rs, ms = groups[w]
-        wait(G_, deps)
-        g.remote_dma_fused([RemoteDMATransfer(dst_ids=[dst(T.cores[r])], dma_engine_mask=mk, remote_sem=T.sem.res,
-                                              srcs=[buf(r)], dsts=[T.RES[:, B * q:B * q + B]])
-                            for r, mk in zip(rs, ms)], local_sem=T.sem.lsem)
-        cnt["ls"] += sum(len(bits(mk)) for mk in ms)
-
-    if not isP:
-        mk = topo.mask(core, pc)
-        wait(G_, [done[3]])
-        send(pc, T.RL[:, 0:96], T.ACC[:, 0:96], "rel1", mk)
-        results("a1", acc, [])
-        wait(G_, [done[4]])
-        send(pc, T.RL[:, 96:192], T.ACC[:, 96:192], "rel2", mk)
-        results("a2", acc, [])
-        fin = []
-        if q <= 3:
-            fin = [do(V_, V.tensor_copy, (T.RES[:, B * q:B * q + B], acc(q)), [done[4]])]
+        last = [done[N - 1]]
+        wait("G", [done[n] for n in range(N)])
+        send(pc, T.RL[:], T.ACC[:], "rel", mrel(q))
+        fin = cp(T.RES[:, col(q)], T.ACC[:, col(q)], last)
+    if is0 or isP:
+        rs = [r for r in range(N) if r != q and near(q, r) != isP]
+        src = T.RL if isP else T.ACC
+        if isP:
+            wait("G", [ext("rel", len(bits(mrel(q))))])
+        mks = split(common(core, [T.cores[r] for r in rs], topo), len(rs))
+        fused([([T.cores[r]], src[:, col(r)], T.RES[:, col(q)], "res", mk) for r, mk in zip(rs, mks)])
+    if is0:
         tot = 0
         for k in range(N):
-            for s, w, rs, ms in result_groups(k, T, topo):
-                tot += sum(len(bits(x)) for r, x in zip(rs, ms) if r == q)
-        f1 = do(V_, V.tensor_tensor, (T.M1[:], T.RES[:, 0:128], T.RES[:, 128:256], A.max), fin + [ext("res", tot)])
-        f2 = do(V_, V.tensor_tensor, (T.M2[:], T.M1[:, 0:64], T.M1[:, 64:128], A.max), [f1])
-        f3 = do(V_, V.tensor_tensor, (T.M3[:], T.M2[:, 0:32], T.M2[:, 32:64], A.max), [f2])
-        f4 = do(V_, V.tensor_scalar, (T.M4[:], T.M3[:], T.THR[:], T.POS[:], A.is_le, A.mult), [f3, m2])
-        f5 = do(V_, V.tensor_tensor, (T.YO[:], T.M3[:], T.M4[:], A.add), [f4])
-        do(SY_, SY.dma_start, (T.y[:], T.YO[:]), [f5], None, 16)
-    else:
-        mg = do(V_, V.tensor_tensor, (T.ACC[:, 128:192], T.ACC[:, 128:192], T.RL[:, 128:192], A.max),
-                [done[2], ext("rel2", nb)])
-        wait(G_, [ext("rel1", nb)])
-        results("p1", rl, [])
-        results("p2", acc, [done[1]])
-        results("p3", lambda r: acc(r) if r >= 4 else rl(r), [done[2], ext("rel2", nb)])
-        results("p4", acc, [mg])
-    g.wait_ge(T.sem.lsem, cnt["ls"])
+            if k != q:
+                s = T.cores[k] if near(k, q) else ports[k]
+                ks = [r for r in range(N) if r != k and near(k, r) == near(k, q)]
+                tot += len(bits(split(common(s, [T.cores[r] for r in ks], topo), len(ks))[0]))
+        f = tt(T.M[:, 0:128], T.RES[:, 0:128], T.RES[:, 128:256], A.max, [fin, ext("res", tot)])
+        f = tt(T.M[:, 128:192], T.M[:, 0:64], T.M[:, 64:128], A.max, [f])
+        f3 = tt(T.M[:, 192:224], T.M[:, 128:160], T.M[:, 160:192], A.max, [f])
+        f = ts(T.M[:, 224:256], T.M[:, 192:224], c_("THR"), A.is_le, [f3, m2], None, c_("POS"), A.mult)
+        f = tt(T.M[:, 256:288], T.M[:, 192:224], T.M[:, 224:256], A.add, [f])
+        do("Y", SY.dma_start, (T.y[:], T.M[:, 256:288]), [f], None, 16)
+    if cnt["ls"]:
+        g.wait_ge(T.sem.lsem, cnt["ls"])
     for e in evs:
         if e["n"] and not any(waited.get((qn, e["k"]), 0) >= e["n"] for qn in eng):
             g.wait_ge(e["sem"], e["n"])

@@ -3,7 +3,8 @@ from concourse.mybir import AluOpType, ActivationFunctionType
 
 N, R, E, B, CAP = 8, 4096, 2048, 32, 512
 MID = R // 2
-NEV = 124
+PRE = 1024
+NEV = 120
 COLS = ["AC", "FC", "J0", "WF", "IV", "KV", "T1", "T2", "ECF", "CW", "NEG", "POS", "THR", "CA", "CB"]
 SLOT = ["GE", "VV", "VW", "VO", "KR", "NJ", "MK", "RK", "PV", "GT", "XO", "SF", "SG"]
 
@@ -18,7 +19,7 @@ for _t, _l in (("float32", dict(win=R + 1, AF=128, FF=128, MI=128, D2=128, ID=12
                                  ON=96, ONB=16, SG=96 * 16))):
     for _n, _w in _l.items():
         SCRATCH[_n] = ("sbuf", [128, _w], _t)
-SEMAPHORES = (["of%d" % h for h in range(N)] + ["fl%d" % h for h in range(N)] + ["res", "lm", "lr", "rel", "lsem", "go"]
+SEMAPHORES = (["of%d" % h for h in range(N)] + ["fl%d" % h for h in range(N)] + ["res", "lm", "lr", "rel0", "rel1", "lsem", "go"]
               + ["e%d" % k for k in range(NEV)])
 
 
@@ -132,6 +133,17 @@ def rank_program(g, core, T, topo):
     tn = lambda r: [plans[s][1][r] for s in range(N) if s != r and near(r, s)]
     tf = lambda r: [plans[s][1][r] for s in range(N) if s != r and not near(r, s)]
     mrel = lambda r: topo.mask(T.cores[r], ports[r]) & common(T.cores[r], tn(r), topo)
+
+    def order_of(r):
+        return [r] + [s for s in range(N) if s != r and near(s, r)] + [s for s in range(N) if s != r and not near(s, r)]
+
+    def blocks(r, far, phase):
+        o = order_of(r)
+        late = lambda b: max(o.index(s) for s in (b - 1, b, b + 1) if 0 <= s < N) > N - 3
+        rs = [s for s in range(N) if s != r and near(r, s) != far and late(s) == bool(phase)]
+        src = ports[r] if far else T.cores[r]
+        return (rs, split(common(src, [T.cores[s] for s in rs], topo), len(rs))) if rs else ([], [])
+
     KC, k0 = (4 if h in (0, N - 1) else 6), max(0, 2 * h - 2)
     W = 16 * KC
 
@@ -139,7 +151,8 @@ def rank_program(g, core, T, topo):
     if is0:
         eI = do("Y", SY.dma_start, (T.MSG[:, 0:16], T.idx[:]), [], None, 16)
         do("V", V.memset, (T.MSG[:, 16:20], 0), [], zc)
-        eE = do("S", S.dma_start, (T.MSG[0:W, 16:17], T.end[:, k0:k0 + KC]), [zc], None, 16)
+        eE = do("Y", SY.dma_start, (T.MSG[0:W, 16:17], T.end[:, k0:k0 + KC]), [zc], None, 16)
+        tabd = [do("Y", SY.dma_start, (T.win[:, 0:PRE], T.tab[:, 0:PRE]), [], None, 16)]
         msgd = [eI, eE, zc]
     else:
         s = T.cores[h] if near(h, q) else ports[h]
@@ -193,9 +206,8 @@ def rank_program(g, core, T, topo):
     e = tt(c_("J0"), c_("T1"), c_("FC"), A.add, [e])
     ts(q_("NJ"), q_("KR"), c_("J0"), A.add, [e], cst, -1.0, A.mult)
     if is0:
-        tabd = [do("Y", SY.dma_start, (T.win[:, 0:512], T.tab[:, 0:512]), [], None, 16)]
         wait("Y", [ext("go", 1), m2])
-        tabd.append(do("Y", SY.dma_start, (T.win[:, 512:MID], T.tab[:, 512:MID]), [], None, 16))
+        tabd.append(do("Y", SY.dma_start, (T.win[:, PRE:MID], T.tab[:, PRE:MID]), [], None, 16))
         tabd.append(do("Y", SY.dma_start, (T.win[:, MID + 1:], T.tab[:, MID:]), [], None, 16))
 
     def late_constants():
@@ -219,36 +231,49 @@ def rank_program(g, core, T, topo):
 
     k2 = None if is0 else late_constants()
 
-    OW, CL, SI, SJ = T.I2[:, 0:16], T.I2[:, 16:32], T.I2[:, 32:48], T.I2[:, 48:80]
-    e = ts(OW, T.MSG[:, 0:16], 12, A.arith_shift_right, msgd)
+    OW, CL, SI = T.I2[:, 0:16], T.I2[:, 16:32], T.I2[:, 32:48]
+    wait("V", msgd)
+    ends = {}
+
+    def end_column():
+        ends["f"] = ts(c_("ECF", W), T.MSG[0:W, 16:17], -float(E * h), A.add, [])
+
+    def end_diagonal():
+        ends["d"] = ts(T.DG[0:W, 0:W], T.ID[0:W, 0:W], c_("ECF", W), A.mult, [ends["f"], k2])
+
+    e = ts(OW, T.MSG[:, 0:16], 12, A.arith_shift_right, [])
+    if not is0:
+        end_column()
     eO = ts(T.O[:], OW, float(q), A.is_equal, [e])
+    if not is0:
+        end_diagonal()
     eIn = do("V", V.tensor_tensor_scan, (T.INC[:], T.ONB[:], T.O[:], 0.0, A.mult, A.add), [eO, m])
+    eC = ts(CL, T.MSG[:, 0:16], R - 1, A.bitwise_and, [])
     eTB = ts(T.TB[:], T.ONB[:], T.INC[:, 15:16], A.mult, [eIn])
+    e = ts(q_("GE"), CL, float(MID), A.is_ge, [eC])
     eX = ev()
     mm(T.pA[:, 0:16], T.A2[:], T.INC[:], True, False, [eIn, cst, eA2], eX)
     mm(T.pA[:, 0:16], T.A32[:], T.O[:], False, False, [eO], eX)
     mm(T.pA[:, 0:16], T.A1[:], T.TB[:], False, True, [eTB], eX)
-    if k2 is None:
+    e = tt(q_("VV"), CL, q_("GE"), A.add, [e])
+    if is0:
         k2 = late_constants()
-    e = ts(c_("ECF", W), T.MSG[0:W, 16:17], -float(E * h), A.add, [])
-    eD = ts(T.DG[0:W, 0:W], T.ID[0:W, 0:W], c_("ECF", W), A.mult, [e, k2])
-    eEF = mm(T.pF[:, 0:W], T.ONF[0:W, :], T.DG[0:W, 0:W], True, True, [eD, m])
+        end_column()
+        end_diagonal()
+    eSI = cp(SI, T.pA[:, 0:16], [eX])
+    e = ts(q_("VW"), q_("VV"), -float(MID), A.add, [e])
+    x = ev()
+    ts(T.I2[:, 48:64], SI, 15, A.bitwise_and, [eSI], x)
+    ts(T.I2[:, 64:80], SI, 4, A.arith_shift_right, [eSI], x)
+    eVO = tt(q_("VO"), q_("VW"), T.O[:], A.mult, [e])
+    eSF = cp(q_("SF", 0, 32), T.I2[:, 48:80], [x])
+    eEF = mm(T.pF[:, 0:W], T.ONF[0:W, :], T.DG[0:W, 0:W], True, True, [ends["d"], m])
     eS = []
     for k in range(0, 16, 2):
         x = ev()
         for t in (k, k + 1):
             do("S", S.activation, (T.SG[:, 96 * t:96 * t + W], T.pF[:, 0:W], SIGN, q_("NJ", t, t + 1)), [eEF, cst], x)
         eS.append(x)
-    e = cp(SI, T.pA[:, 0:16], [eX])
-    x = ev()
-    ts(T.I2[:, 48:64], SI, 15, A.bitwise_and, [e], x)
-    ts(T.I2[:, 64:80], SI, 4, A.arith_shift_right, [e], x)
-    eSF = cp(q_("SF", 0, 32), SJ, [x])
-    eC = ts(CL, T.MSG[:, 0:16], R - 1, A.bitwise_and, [])
-    e = ts(q_("GE"), CL, float(MID), A.is_ge, [eC])
-    e = tt(q_("VV"), CL, q_("GE"), A.add, [e])
-    e = ts(q_("VW"), q_("VV"), -float(MID), A.add, [e])
-    eVO = tt(q_("VO"), q_("VW"), T.O[:], A.mult, [e])
     eP, eCn = ev(), ev()
     mm(T.pC[0:W, 0:1], T.ON[:, 0:W], T.INC[:, 15:16], True, False, [m], eCn)
     for k in range(0, 16, 2):
@@ -260,39 +285,49 @@ def rank_program(g, core, T, topo):
             mm(T.pB[:, 0:32], T.LH[:, 128 * t:128 * t + 128], T.RH[:, 32 * t:32 * t + 32], t == 0, t == 15, [x], eP)
             mm(T.pC[0:W, 0:1], T.SG[:, 96 * t:96 * t + W], T.O[:, t:t + 1], False, t == 15, [eS[k // 2]], eCn)
     eA = ts(T.OUTA[:], T.pB[:, 0:32], float(MID), A.add, [eP])
-    mrep = topo.mask(core, c0)
-    nrep = lambda c: len(bits(topo.mask(c, c0)))
+    nrep = lambda c: topo.mask(c, c0) & mrel(q)
     if not is0:
         wait("G", [eA])
-        send(c0, T.OF[:, 40 * h:40 * h + 32], T.OUTA[:], "of%d" % h, mrep)
+        send(c0, T.OF[:, 40 * h:40 * h + 32], T.OUTA[:], "of%d" % h, nrep(core))
     e = ts(c_("CW", W), T.pC[0:W, 0:1], 0.5, A.mult, [eCn, m])
-    eOH = ts(T.OHF[:], T.IOT[:], c_("CW"), A.is_equal, [e, k2, m])
+    eFM = ev()
+    half = [(slice(0, 256), T.pE[:, 0:256]), (slice(256, 512), T.pA[:, 256:512])]
+    oh = [ts(T.OHF[:, sl], T.IOT[:, sl], c_("CW"), A.is_equal, [e, k2, m]) for sl, ps in half]
     eRK = ts(q_("RK", 1, 1 + KC, W), q_("MK", 0, KC, W), c_("CW", W), A.mult, [e, k2, m])
-    eFl = mm(T.pE[:], T.NB[:], T.OHF[:], True, True, [eOH, m2])
+    for (sl, ps), o in zip(half, oh):
+        x = mm(ps, T.NB[:], T.OHF[:, sl], True, True, [o, m2, eSI])
+        do("S", S.activation, (T.FLM[:, sl], ps, COPY), [x], eFM)
     eR = ev()
     rk, rk1 = q_("RK", 1, 1 + KC, W), q_("RK", 0, KC, W)
     mm(T.pD[:, 0:KC], T.CREP[0:W, :], rk, True, True, [eRK], eR)
     mm(T.pD[:, 8:8 + KC], T.CSH[0:W, :], rk, True, False, [], eR)
     mm(T.pD[:, 8:8 + KC], T.CWR[0:W, :], rk1, False, True, [], eR)
-    eFM = do("S", S.activation, (T.FLM[:], T.pE[:], COPY), [eFl])
     e = cp(q_("PV", 0, KC), T.pD[:, 8:8 + KC], [eR])
     e = tt(q_("GT", 0, KC), T.pD[:, 0:KC], q_("PV", 0, KC), A.is_gt, [e])
     e = tt(q_("XO", 0, KC), T.pD[:, 0:KC], q_("GT", 0, KC), A.mult, [e])
     eC2 = cp(T.OUTC[:, 0:KC], q_("XO", 0, KC), [e, m])
     if not is0:
         wait("G", [eFM])
-        send(c0, T.FL[:, CAP * h:CAP * h + CAP], T.FLM[:], "fl%d" % h, mrep)
+        send(c0, T.FL[:, CAP * h:CAP * h + CAP], T.FLM[:], "fl%d" % h, nrep(core))
         wait("G", [eC2])
-        send(c0, T.OF[:, 40 * h + 32:40 * h + 40], T.OUTC[:], "fl%d" % h, mrep)
+        send(c0, T.OF[:, 40 * h + 32:40 * h + 40], T.OUTC[:], "fl%d" % h, nrep(core))
 
     col = lambda r: slice(B * r, B * r + B)
+
+    def results(phase):
+        rs, ms = blocks(q, True, phase)
+        if rs:
+            fused([([pc], T.ACC[:, col(r)], T.RL[:, col(r)], "rel%d" % phase, mk) for r, mk in zip(rs, split(mrel(q), len(rs)))])
+        rs, ms = blocks(q, False, phase)
+        if rs:
+            fused([([T.cores[r]], T.ACC[:, col(r)], T.RES[:, col(q)], "res", mk) for r, mk in zip(rs, ms)])
+
     if is0:
         eY = ev()
         for k in range(2):
             cp(T["Y%d" % k][:, 0:1], c_("NEG"), [m2], eY)
-        order = [q] + [r for r in range(N) if r != q and near(r, q)] + [r for r in range(N) if r != q and not near(r, q)]
         scn, done = {}, {}
-        for n, r in enumerate(order):
+        for n, r in enumerate(order_of(q)):
             X, Y = T["X%d" % (n % 3)], T["Y%d" % (n % 2)]
             kc, kk = (4 if r in (0, N - 1) else 6), max(0, 2 * r - 2)
             if r == q:
@@ -300,31 +335,31 @@ def rank_program(g, core, T, topo):
             else:
                 off, fl = T.OF[:, 40 * r:40 * r + 32], T.FL[:, CAP * r:CAP * r + CAP]
                 xo = T.OF[:, 40 * r + 32:40 * r + 32 + kc]
-                d1, d2 = [ext("of%d" % r, nrep(plans[q][1][r]))], [ext("fl%d" % r, 2 * nrep(plans[q][1][r]))]
+                ne = len(bits(nrep(plans[q][1][r])))
+                d1, d2 = [ext("of%d" % r, ne)], [ext("fl%d" % r, 2 * ne)]
             ga = do("S", S.activation, (X[:], T.win[:].indirect(off), COPY), tabd + [m2] + d1 + ([scn[n - 3]] if n > 2 else []))
             scn[n] = do("V", V.tensor_tensor_scan, (Y[:, 1:], fl, X[:], c_("NEG"), A.min, A.max),
                         [ga, m2, eY] + d2 + ([done[n - 2]] if n > 1 else []))
             acc = T.ACC[:, 16 * kk:16 * kk + 16 * kc]
             done[n] = tt(acc, Y[:].indirect(xo), acc, A.max, [scn[n]] + ([done[n - 1]] if n else []))
 
-        last = [done[N - 1]]
-        wait("G", [done[n] for n in range(N)])
-        send(pc, T.RL[:], T.ACC[:], "rel", mrel(q))
-        fin = cp(T.RES[:, col(q)], T.ACC[:, col(q)], last)
-    if is0 or isP:
-        rs = [r for r in range(N) if r != q and near(q, r) != isP]
-        src = T.RL if isP else T.ACC
-        if isP:
-            wait("G", [ext("rel", len(bits(mrel(q))))])
-        mks = split(common(core, [T.cores[r] for r in rs], topo), len(rs))
-        fused([([T.cores[r]], src[:, col(r)], T.RES[:, col(q)], "res", mk) for r, mk in zip(rs, mks)])
+        wait("G", [done[n] for n in range(N - 2)])
+        results(0)
+        wait("G", [done[N - 2], done[N - 1]])
+        results(1)
+        fin = cp(T.RES[:, col(q)], T.ACC[:, col(q)], [done[N - 1]])
+    if isP:
+        for phase in (0, 1):
+            rs, ms = blocks(q, True, phase)
+            if rs:
+                wait("G", [ext("rel%d" % phase, sum(len(bits(x)) for x in split(mrel(q), len(rs))))])
+                fused([([T.cores[r]], T.RL[:, col(r)], T.RES[:, col(q)], "res", mk) for r, mk in zip(rs, ms)])
     if is0:
         tot = 0
         for k in range(N):
-            if k != q:
-                s = T.cores[k] if near(k, q) else ports[k]
-                ks = [r for r in range(N) if r != k and near(k, r) == near(k, q)]
-                tot += len(bits(split(common(s, [T.cores[r] for r in ks], topo), len(ks))[0]))
+            for far in (True, False):
+                for phase in (0, 1):
+                    tot += sum(len(bits(mk)) for r, mk in zip(*blocks(k, far, phase)) if r == q)
         f = tt(T.M[:, 0:128], T.RES[:, 0:128], T.RES[:, 128:256], A.max, [fin, ext("res", tot)])
         f = tt(T.M[:, 128:192], T.M[:, 0:64], T.M[:, 64:128], A.max, [f])
         f3 = tt(T.M[:, 192:224], T.M[:, 128:160], T.M[:, 160:192], A.max, [f])

@@ -1,26 +1,27 @@
 from concourse.bass import DstId, RemoteDMATransfer
-from concourse.mybir import AluOpType, ActivationFunctionType
+from concourse.mybir import AluOpType, ActivationFunctionType, AxisListType
 
 N, R, E, B, CAP = 8, 4096, 2048, 32, 512
 MID = R // 2
-PRE = 1024
-NEV = 120
-COLS = ["AC", "FC", "J0", "WF", "IV", "KV", "T1", "T2", "ECF", "CW", "NEG", "POS", "THR", "CA", "CB"]
-SLOT = ["GE", "VV", "VW", "VO", "KR", "NJ", "MK", "RK", "PV", "GT", "XO", "SF", "SG"]
+PRE = 1280
+NEV = 112
+DIRECT = 4
+COLS = ["AC", "FC", "WF", "IV", "KV", "T2", "CW", "NEG", "POS", "THR", "CA", "CB", "PC", "F3", "F3b", "F3c"]
+SLOT = ["GE", "VW", "VO", "MK", "RK", "PV", "GT", "XO", "S1", "HF", "H16", "KOH", "Z"]
 
-SCRATCH = {"p%s" % k: ("psum", [128, 512], "float32") for k in "ABCDEF"}
-for _t, _l in (("float32", dict(win=R + 1, AF=128, FF=128, MI=128, D2=128, ID=128, DG=96, ONF=128, CREP=128, CSH=128, CWR=128,
-                                TA=128, TB2=128, S=16, Q=16 * len(SLOT), ACC=256, RL=256, RES=256, M=288,
-                                X0=CAP, X1=CAP, X2=CAP, Y0=CAP + 1, Y1=CAP + 1)),
-               ("int32", dict(MSG=20, RLY=20, IOI=CAP, I1=4, I2=80)),
+SCRATCH = {"p%s" % k: ("psum", [128, 512], "float32") for k in "ABCDEFG"}
+for _t, _l in (("float32", dict(win=R + 1, AF=128, FF=128, MI=128, IDF=96, ONF=128, CREP=128, CSH=128, CWR=128, IOF=128,
+                                TB2=128, TA=128, S=16, Q=16 * len(SLOT), ACC=256, RL=256, RL1=256, RES=256, M=288,
+                                X0=CAP, X1=CAP, X2=CAP, Y0=CAP + 1, Y1=CAP + 1, Y2=CAP + 1)),
+               ("int32", dict(MSG=20, RLY=20, I1=4, I2=48, I3=4)),
                ("uint16", dict(IM=128, IC=32, IOT=CAP, OUTA=32, OUTC=8, OF=40 * N)),
-               ("float16", dict(LH=128 * 16, RH=32 * 16)),
+               ("float16", dict(LH=128 * 16, RH=32 * 16, SI=16, OHP=96)),
                ("bfloat16", dict(NB0=128, NB=128, OHF=CAP, FLM=CAP, FL=CAP * N, A1=128, A2=128, A32=128, O=16, INC=16, TB=16,
-                                 ON=96, ONB=16, SG=96 * 16))):
+                                 ON=128, ONB=16, ID=96, DG=96))):
     for _n, _w in _l.items():
         SCRATCH[_n] = ("sbuf", [128, _w], _t)
-SEMAPHORES = (["of%d" % h for h in range(N)] + ["fl%d" % h for h in range(N)] + ["res", "lm", "lr", "rel0", "rel1", "lsem", "go"]
-              + ["e%d" % k for k in range(NEV)])
+SEMAPHORES = (["of%d" % h for h in range(N)] + ["fl%d" % h for h in range(N)] + ["xo%d" % h for h in range(N)]
+              + ["res", "lm", "lr", "rel0", "rel1", "lsem", "go"] + ["e%d" % k for k in range(NEV)])
 
 
 def bits(m):
@@ -64,14 +65,14 @@ def rank_program(g, core, T, topo):
     is0, isP = core == c0, core == pc
     near = lambda r, s: topo.may_write(T.cores[r], T.cores[s])
     A = AluOpType
-    COPY, SIGN = ActivationFunctionType.Copy, ActivationFunctionType.Sign
+    COPY = ActivationFunctionType.Copy
     V, S, PE, SY = g.vector, g.scalar, g.tensor, g.sync
     eng = {"V": V, "S": S, "P": PE, "Y": SY, "G": g}
     evs, waited, cnt = [], {}, {"ls": 0}
 
-    def c_(name, P=128):
+    def c_(name, P=128, w=1):
         k = COLS.index(name)
-        return T.S[0:P, k:k + 1]
+        return T.S[0:P, k:k + w]
 
     def q_(name, a=0, b=16, P=128):
         k = 16 * SLOT.index(name)
@@ -130,12 +131,21 @@ def rank_program(g, core, T, topo):
                            local_sem=T.sem.lsem)
         cnt["ls"] += sum(len(bits(x[4])) for x in trs)
 
-    tn = lambda r: [plans[s][1][r] for s in range(N) if s != r and near(r, s)]
-    tf = lambda r: [plans[s][1][r] for s in range(N) if s != r and not near(r, s)]
-    mrel = lambda r: topo.mask(T.cores[r], ports[r]) & common(T.cores[r], tn(r), topo)
+    kin = lambda r: [s for s in range(N) if s == r or near(r, s)]
+    turn = lambda r, s: (kin(s).index(s) - kin(r).index(r)) % len(kin(s))
+    tabs = lambda r, nr: sorted([s for s in range(N) if s != r and near(r, s) == nr], key=lambda s: turn(r, s))
+    tn = lambda r: [plans[s][1][r] for s in tabs(r, True)]
+    tf = lambda r: [plans[s][1][r] for s in tabs(r, False)]
+    mnear = lambda r: topo.mask(T.cores[r], ports[r]) & common(T.cores[r], tn(r), topo)
+    mrel = lambda r: topo.mask(T.cores[r], ports[r]) & ~mnear(r) or mnear(r)
 
     def order_of(r):
-        return [r] + [s for s in range(N) if s != r and near(s, r)] + [s for s in range(N) if s != r and not near(s, r)]
+        come = lambda nr: sorted([s for s in range(N) if s != r and near(s, r) == nr], key=lambda s: turn(s, r))
+        fr = come(False)
+        own = lambda t, nr: len([b for b in range(N) if b != r and near(r, b) == nr and any(abs(b - s) < 2 for s in t)])
+        last = min([(a, b) for a in fr for b in fr if fr.index(a) < fr.index(b)],
+                   key=lambda t: (own(t, False), own(t, True), -fr.index(t[0]) - fr.index(t[1])))
+        return [r] + come(True) + [s for s in fr if s not in last] + list(last)
 
     def blocks(r, far, phase):
         o = order_of(r)
@@ -157,191 +167,210 @@ def rank_program(g, core, T, topo):
     else:
         s = T.cores[h] if near(h, q) else ports[h]
         msgd = [ext("lm", len(bits(common(s, tn(h) if near(h, q) else tf(h), topo))))]
-    c1 = ev()
+    c1, c1b = ev(), ev()
     iota(T.I1[:, 0:1], [[0, 1]], 0, 1, c1)
     iota(T.AF[:], [[0, 16], [1, 8]], 0, 0, c1)
     iota(T.FF[:], [[1, 16], [0, 8]], 0, 0, c1)
     iota(T.MI[:], [[0, 8], [1, 16]], 0, 0, c1)
-    iota(q_("KR"), [[16, 16]], 0, 0, c1)
+    iota(c_("WF"), [[0, 1]], 0, 1, c1b)
     if is0:
         wait("G", msgd)
         send(pc, T.RLY[:], T.MSG[:], "lr", mrel(q))
         fused([(tn(q), T.MSG[:], T.MSG[:], "lm", common(core, tn(q), topo))])
         g.sem_inc(T.sem.go, 1)
-    c2 = ev()
-    iota(T.ID[0:96, 0:96], [[1, 96]], 0, -1, c2)
-    iota(T.D2[0:W, :], [[0, 8], [KC, 16]], 0, -1, c2)
-    iota(T.IOI[:], [[1, CAP]], 0, 0, c2)
-    iota(c_("WF"), [[0, 1]], 0, 1, c2)
+    iota(T.IDF[0:96, 0:96], [[1, 96]], 0, -1, c1b)
     if isP:
         wait("G", [ext("lr", len(bits(mrel(q))))])
         fused([(tf(q), T.RLY[:], T.MSG[:], "lm", common(core, tf(q), topo))])
+    c2 = ev()
+    iota(T.IOF[:], [[1, 128]], 0, 0, c2)
 
     m = ev()
-    for ap, v in ((c_("CA"), -9e29), (c_("CB"), -7.5e29), (T.NB0[0:96, :], -9e29), (T.NB0[96:128, :], 1.4e28),
-                  (c_("CW"), 5000.0), (T.IOT[96:128, :], 5000), (q_("RK"), 0.0), (T.OUTC[:], 0),
-                  (T.ONB[:], 1.0), (T.ON[:], 1.0), (T.ONF[:], 1.0)) + (((T.ACC[:], -9e29),) if is0 else ()):
+    for ap, v in ((T.ONB[:], 1.0), (T.ON[:], 1.0), (c_("CA"), -9e29), (T.ONF[:], 1.0)):
         do("V", V.memset, (ap, v), [], m)
-    m2 = ev()
-    for o, i, s in ((c_("NEG"), c_("CA"), 2.0), (c_("POS"), c_("CA"), -2.0), (c_("THR"), c_("CB"), 2.0),
-                    (T.NB[:], T.NB0[:], 4.0), (T.win[:, MID:MID + 1], c_("CA"), 2.0)) + (
-                        ((T.ACC[:], T.ACC[:], 2.0),) if is0 else ()):
-        ts(o, i, s, A.mult, [m], m2)
+
+    def select(out, i, base, up, op, deps, e=None):
+        s = 1 if up else -1
+        return do("G", g.affine_select, (out, i, [[0, 8], [s * KC, 16]], op, 0.0, base, -s), deps, e)
+
+    c3 = ev()
+    x1 = select(T.CREP[0:W, :], T.ONF[0:W, :], KC, True, A.is_gt, [m])
+    x2 = select(T.CSH[0:W, :], T.ONF[0:W, :], 0, True, A.is_gt, [m])
+    select(T.CWR[0:W, :], T.ONF[0:W, :], -15 * KC, False, A.is_ge, [m], c3)
+    select(T.CREP[0:W, :], T.CREP[0:W, :], 0, False, A.is_ge, [x1], c3)
+    select(T.CSH[0:W, :], T.CSH[0:W, :], KC, False, A.is_ge, [x2], c3)
+
     a = ev()
     ts(T.I1[:, 1:2], T.I1[:, 0:1], 7, A.bitwise_and, [c1], a)
     ts(T.I1[:, 2:3], T.I1[:, 0:1], 3, A.arith_shift_right, [c1], a)
+    mb = ev()
+    for ap, v in ((c_("CW"), 5000.0), (q_("RK"), 0.0), (T.OUTC[:], 0)):
+        do("V", V.memset, (ap, v), [], mb)
     b = ev()
     cp(c_("AC"), T.I1[:, 1:2], [a], b)
     cp(c_("FC"), T.I1[:, 2:3], [a], b)
-    cst = ev()
-    cp(T.IM[:], T.MI[:], [c1], cst)
-    cp(T.IC[:, 0:16], T.MI[:, 0:16], [c1], cst)
-    ts(T.IC[:, 16:32], T.MI[:, 0:16], 16.0, A.add, [c1], cst)
-    ts(T.A1[:], T.AF[:], c_("AC"), A.is_gt, [b], cst)
-    eA2 = ts(T.A2[:], T.AF[:], c_("AC"), A.is_equal, [b])
-    e = ts(T.TA[:], T.FF[:], c_("FC"), A.is_gt, [b])
-    e = tt(T.TB2[:], T.TA[:], T.A2[:], A.mult, [e, eA2])
-    tt(T.A32[:], T.TB2[:], T.A2[:], A.subtract, [e], cst)
-    e = ts(c_("T1"), c_("AC"), 256.0, A.mult, [b], None, 0.5, A.add)
-    e = tt(c_("J0"), c_("T1"), c_("FC"), A.add, [e])
-    ts(q_("NJ"), q_("KR"), c_("J0"), A.add, [e], cst, -1.0, A.mult)
+    m2 = ev()
+    ts(c_("NEG"), c_("CA"), 2.0, A.mult, [m], m2)
     if is0:
+        ts(T.win[:, MID:MID + 1], c_("CA"), 2.0, A.mult, [m], m2)
         wait("Y", [ext("go", 1), m2])
         tabd.append(do("Y", SY.dma_start, (T.win[:, PRE:MID], T.tab[:, PRE:MID]), [], None, 16))
         tabd.append(do("Y", SY.dma_start, (T.win[:, MID + 1:], T.tab[:, MID:]), [], None, 16))
+    cst = ev()
+    eA2 = ts(T.A2[:], T.AF[:], c_("AC"), A.is_equal, [b])
+    e = ts(T.TA[:], T.FF[:], c_("FC"), A.is_gt, [b])
+    ts(T.A1[:], T.AF[:], c_("AC"), A.is_gt, [b], cst)
+    e = tt(T.TB2[:], T.TA[:], T.A2[:], A.mult, [e, eA2])
+    cp(T.IM[:], T.MI[:], [c1], cst)
+    cp(T.IC[:, 0:16], T.MI[:, 0:16], [c1], cst)
+    ts(T.IC[:, 16:32], T.MI[:, 0:16], 16.0, A.add, [c1], cst)
+    tt(T.A32[:], T.TB2[:], T.A2[:], A.subtract, [e], cst)
+
+    k2 = ev()
 
     def late_constants():
-        k = ev()
-        ts(T.ID[0:96, 0:96], T.ID[0:96, 0:96], 0.0, A.is_equal, [c2], k)
-        cp(T.IOT[0:96, :], T.IOI[0:96, :], [c2, m], k)
-        x = ev()
-        ts(T.CREP[0:W, :], T.D2[0:W, :], -float(KC), A.is_gt, [c2], x)
-        ts(T.CSH[0:W, :], T.D2[0:W, :], 0.0, A.is_gt, [c2], x)
-        ts(T.TA[0:W, :], T.D2[0:W, :], 0.0, A.is_le, [c2, cst], x)
-        ts(T.TB2[0:W, :], T.D2[0:W, :], float(KC), A.is_le, [c2, cst], x)
-        ts(T.CWR[0:W, :], T.D2[0:W, :], -15.0 * KC, A.is_le, [c2], k)
-        tt(T.CREP[0:W, :], T.CREP[0:W, :], T.TA[0:W, :], A.mult, [x], k)
-        tt(T.CSH[0:W, :], T.CSH[0:W, :], T.TB2[0:W, :], A.mult, [x], k)
-        e = ts(c_("T2"), c_("WF"), 1.0 / KC, A.mult, [c2], None, -0.5 + 0.5 / KC, A.add)
-        e = cp(T.I1[:, 3:4], c_("T2"), [e])
-        e = cp(c_("IV"), T.I1[:, 3:4], [e])
-        e = ts(c_("KV"), c_("IV"), -float(KC), A.mult, [e], None, c_("WF"), A.add)
-        ts(q_("MK", 0, 8), T.IC[:, 0:8], c_("KV"), A.is_equal, [e, cst], k)
-        return k
+        z = ev()
+        for ap, v in ((T.NB0[0:96, :], -9e29), (T.NB0[96:128, :], 1.4e28), (T.IOT[96:128, :], 5000)) + (
+                ((T.ACC[:], -9e29), (c_("CB"), -7.5e29)) if is0 else ()):
+            do("V", V.memset, (ap, v), [], z)
+        e1 = ts(c_("T2"), c_("WF"), 1.0 / KC, A.mult, [c1b], None, -0.5 + 0.5 / KC, A.add)
+        i0 = cp(T.IOT[0:96, 0:128], T.IOF[0:96, :], [c2])
+        e2 = cp(T.I1[:, 3:4], c_("T2"), [e1])
+        ts(T.NB[:], T.NB0[:], 4.0, A.mult, [z], k2)
+        e3 = cp(c_("IV"), T.I1[:, 3:4], [e2])
+        for k in (1, 2, 3):
+            ts(T.IOT[0:96, 128 * k:128 * k + 128], T.IOT[0:96, 0:128], 128.0 * k, A.add, [i0], k2)
+        e4 = ts(c_("KV"), c_("IV"), -float(KC), A.mult, [e3], None, c_("WF"), A.add)
+        if is0:
+            ts(T.ACC[:], T.ACC[:], 2.0, A.mult, [z], k2)
+            for k in range(3):
+                cp(T["Y%d" % k][:, 0:1], c_("NEG"), [m2], k2)
+            ts(c_("POS"), c_("CA"), -2.0, A.mult, [m], k2)
+            ts(c_("THR"), c_("CB"), 2.0, A.mult, [z], k2)
+        ts(q_("MK", 0, 8), T.IC[:, 0:8], c_("KV"), A.is_equal, [e4, cst], k2)
 
-    k2 = None if is0 else late_constants()
+    if not is0:
+        late_constants()
+    idd = ts(T.ID[0:96, 0:96], T.IDF[0:96, 0:96], 0.0, A.is_equal, [c1b]) if not is0 else None
 
-    OW, CL, SI = T.I2[:, 0:16], T.I2[:, 16:32], T.I2[:, 32:48]
+    OW, CL, HI = T.I2[:, 0:16], T.I2[:, 16:32], T.I2[:, 32:48]
     wait("V", msgd)
-    ends = {}
-
-    def end_column():
-        ends["f"] = ts(c_("ECF", W), T.MSG[0:W, 16:17], -float(E * h), A.add, [])
-
-    def end_diagonal():
-        ends["d"] = ts(T.DG[0:W, 0:W], T.ID[0:W, 0:W], c_("ECF", W), A.mult, [ends["f"], k2])
-
-    e = ts(OW, T.MSG[:, 0:16], 12, A.arith_shift_right, [])
-    if not is0:
-        end_column()
-    eO = ts(T.O[:], OW, float(q), A.is_equal, [e])
-    if not is0:
-        end_diagonal()
+    eOW = ts(OW, T.MSG[:, 0:16], 12, A.arith_shift_right, [])
+    eE1 = ts(T.I3[0:W, 3:4], T.MSG[0:W, 16:17], -float(E * h + 1), A.add, [], None, float(E - 1), A.min)
+    eCL = ts(CL, T.MSG[:, 0:16], R - 1, A.bitwise_and, [])
+    eO = ts(T.O[:], OW, float(q), A.is_equal, [eOW])
+    eI3 = ev()
+    ts(T.I3[0:W, 0:1], T.I3[0:W, 3:4], 15, A.bitwise_and, [eE1], eI3)
     eIn = do("V", V.tensor_tensor_scan, (T.INC[:], T.ONB[:], T.O[:], 0.0, A.mult, A.add), [eO, m])
-    eC = ts(CL, T.MSG[:, 0:16], R - 1, A.bitwise_and, [])
+    ts(T.I3[0:W, 1:2], T.I3[0:W, 3:4], 8, A.arith_shift_right, [], eI3)
+    do("V", V.tensor_scalar, (T.I3[0:W, 2:3], T.I3[0:W, 3:4], 4, 15, A.arith_shift_right, A.bitwise_and), [], eI3)
     eTB = ts(T.TB[:], T.ONB[:], T.INC[:, 15:16], A.mult, [eIn])
-    e = ts(q_("GE"), CL, float(MID), A.is_ge, [eC])
     eX = ev()
     mm(T.pA[:, 0:16], T.A2[:], T.INC[:], True, False, [eIn, cst, eA2], eX)
     mm(T.pA[:, 0:16], T.A32[:], T.O[:], False, False, [eO], eX)
     mm(T.pA[:, 0:16], T.A1[:], T.TB[:], False, True, [eTB], eX)
-    e = tt(q_("VV"), CL, q_("GE"), A.add, [e])
+    eF3 = ts(c_("F3", W, 3), T.I3[0:W, 0:3], -0.5, A.max, [eI3])
+    eGE = ts(q_("GE"), CL, float(MID), A.is_ge, [eCL], None, -float(MID), A.add)
     if is0:
-        k2 = late_constants()
-        end_column()
-        end_diagonal()
-    eSI = cp(SI, T.pA[:, 0:16], [eX])
-    e = ts(q_("VW"), q_("VV"), -float(MID), A.add, [e])
-    x = ev()
-    ts(T.I2[:, 48:64], SI, 15, A.bitwise_and, [eSI], x)
-    ts(T.I2[:, 64:80], SI, 4, A.arith_shift_right, [eSI], x)
-    eVO = tt(q_("VO"), q_("VW"), T.O[:], A.mult, [e])
-    eSF = cp(q_("SF", 0, 32), T.I2[:, 48:80], [x])
-    eEF = mm(T.pF[:, 0:W], T.ONF[0:W, :], T.DG[0:W, 0:W], True, True, [ends["d"], m])
-    eS = []
+        idd = ts(T.ID[0:96, 0:96], T.IDF[0:96, 0:96], 0.0, A.is_equal, [c1b])
+    ePC = ts(c_("PC", W), c_("F3", W), 8.0, A.mult, [eF3], None, c_("F3b", W), A.add)
+    eVW = tt(q_("VW"), CL, q_("GE"), A.add, [eGE])
+    eSl = ev()
+    ts(HI, T.pA[:, 0:16], -7.5, A.add, [eX], eSl, 1.0 / 16, A.mult)
+    cp(q_("S1"), T.pA[:, 0:16], [], eSl)
+    eVO = tt(q_("VO"), q_("VW"), T.O[:], A.mult, [eVW])
+    eHF = ev()
+    cp(q_("HF"), HI, [eSl], eHF)
+    ts(q_("H16"), HI, 16.0, A.mult, [], eHF)
+    eSI = tt(T.SI[:], T.pA[:, 0:16], T.O[:], A.add, [])
+    eDG = ts(T.DG[0:W, 0:W], T.ID[0:W, 0:W], c_("PC", W), A.mult, [ePC, idd])
+    ePF = mm(T.pF[:, 0:W], T.ON[0:W, :], T.DG[0:W, 0:W], True, True, [eDG, m])
+    eP = ev()
     for k in range(0, 16, 2):
         x = ev()
         for t in (k, k + 1):
-            do("S", S.activation, (T.SG[:, 96 * t:96 * t + W], T.pF[:, 0:W], SIGN, q_("NJ", t, t + 1)), [eEF, cst], x)
-        eS.append(x)
-    eP, eCn = ev(), ev()
-    mm(T.pC[0:W, 0:1], T.ON[:, 0:W], T.INC[:, 15:16], True, False, [m], eCn)
-    for k in range(0, 16, 2):
-        x = ev()
-        for t in (k, k + 1):
-            ts(T.LH[:, 128 * t:128 * t + 128], T.IM[:], q_("SF", t, t + 1), A.is_equal, [eSF, cst], x)
-            ts(T.RH[:, 32 * t:32 * t + 32], T.IC[:], q_("SF", 16 + t, 17 + t), A.is_equal, [eVO], x, q_("VO", t, t + 1), A.mult)
+            ts(T.LH[:, 128 * t:128 * t + 128], T.IM[:], q_("H16", t, t + 1), A.add, [eHF, cst], x, q_("S1", t, t + 1), A.is_equal)
+            ts(T.RH[:, 32 * t:32 * t + 32], T.IC[:], q_("HF", t, t + 1), A.is_equal, [eVO], x, q_("VO", t, t + 1), A.mult)
         for t in (k, k + 1):
             mm(T.pB[:, 0:32], T.LH[:, 128 * t:128 * t + 128], T.RH[:, 32 * t:32 * t + 32], t == 0, t == 15, [x], eP)
-            mm(T.pC[0:W, 0:1], T.SG[:, 96 * t:96 * t + W], T.O[:, t:t + 1], False, t == 15, [eS[k // 2]], eCn)
+        if k == 2:
+            oh = ts(T.OHP[:, 0:W], T.pF[:, 0:W], c_("WF"), A.is_equal, [ePF, c1b])
+            pk = mm(T.pC[0:W, 0:16], T.OHP[:, 0:W], T.SI[:], True, True, [oh, eSI])
+        if k == 6:
+            kh = ts(q_("KOH", P=W), T.IC[0:W, 0:16], c_("F3c", W), A.is_equal, [cst])
+        if k == 8:
+            z = tt(q_("Z", P=W), T.pC[0:W, 0:16], q_("KOH", P=W), A.mult, [pk, kh])
+        if k == 10:
+            eCW = do("V", V.tensor_reduce, (c_("CW", W), q_("Z", P=W), AxisListType.X, A.add), [z, mb])
+    if is0:
+        late_constants()
+    eFM = ev()
+    if is0:
+        o = ts(T.OHF[:], T.IOT[:], c_("CW"), A.is_equal, [eCW, k2])
+        mm(T.pE[:], T.NB[:], T.OHF[:], True, True, [o], eFM)
+    else:
+        half = [(slice(0, 256), T.pE[:, 0:256]), (slice(256, 512), T.pG[:, 0:256])]
+        for sl, ps in half:
+            o = ts(T.OHF[:, sl], T.IOT[:, sl], c_("CW"), A.is_equal, [eCW, k2])
+            x = mm(ps, T.NB[:], T.OHF[:, sl], True, True, [o])
+            do("S", S.activation, (T.FLM[:, sl], ps, COPY), [x], eFM)
     eA = ts(T.OUTA[:], T.pB[:, 0:32], float(MID), A.add, [eP])
-    nrep = lambda c: topo.mask(c, c0) & mrel(q)
+    nrep = lambda c: topo.mask(c, c0) & mnear(q)
     if not is0:
         wait("G", [eA])
         send(c0, T.OF[:, 40 * h:40 * h + 32], T.OUTA[:], "of%d" % h, nrep(core))
-    e = ts(c_("CW", W), T.pC[0:W, 0:1], 0.5, A.mult, [eCn, m])
-    eFM = ev()
-    half = [(slice(0, 256), T.pE[:, 0:256]), (slice(256, 512), T.pA[:, 256:512])]
-    oh = [ts(T.OHF[:, sl], T.IOT[:, sl], c_("CW"), A.is_equal, [e, k2, m]) for sl, ps in half]
-    eRK = ts(q_("RK", 1, 1 + KC, W), q_("MK", 0, KC, W), c_("CW", W), A.mult, [e, k2, m])
-    for (sl, ps), o in zip(half, oh):
-        x = mm(ps, T.NB[:], T.OHF[:, sl], True, True, [o, m2, eSI])
-        do("S", S.activation, (T.FLM[:, sl], ps, COPY), [x], eFM)
-    eR = ev()
     rk, rk1 = q_("RK", 1, 1 + KC, W), q_("RK", 0, KC, W)
-    mm(T.pD[:, 0:KC], T.CREP[0:W, :], rk, True, True, [eRK], eR)
-    mm(T.pD[:, 8:8 + KC], T.CSH[0:W, :], rk, True, False, [], eR)
+    eRK = ts(rk, q_("MK", 0, KC, W), c_("CW", W), A.mult, [eCW, k2, mb])
+    eR = ev()
+    mm(T.pD[:, 8:8 + KC], T.CSH[0:W, :], rk, True, False, [eRK, c3], eR)
     mm(T.pD[:, 8:8 + KC], T.CWR[0:W, :], rk1, False, True, [], eR)
+    mm(T.pD[:, 0:KC], T.CREP[0:W, :], rk, True, True, [], eR)
     e = cp(q_("PV", 0, KC), T.pD[:, 8:8 + KC], [eR])
     e = tt(q_("GT", 0, KC), T.pD[:, 0:KC], q_("PV", 0, KC), A.is_gt, [e])
     e = tt(q_("XO", 0, KC), T.pD[:, 0:KC], q_("GT", 0, KC), A.mult, [e])
-    eC2 = cp(T.OUTC[:, 0:KC], q_("XO", 0, KC), [e, m])
+    eC2 = cp(T.OUTC[:, 0:KC], q_("XO", 0, KC), [e, mb])
     if not is0:
         wait("G", [eFM])
         send(c0, T.FL[:, CAP * h:CAP * h + CAP], T.FLM[:], "fl%d" % h, nrep(core))
         wait("G", [eC2])
-        send(c0, T.OF[:, 40 * h + 32:40 * h + 40], T.OUTC[:], "fl%d" % h, nrep(core))
+        send(c0, T.OF[:, 40 * h + 32:40 * h + 40], T.OUTC[:], "xo%d" % h, nrep(core))
 
     col = lambda r: slice(B * r, B * r + B)
 
     def results(phase):
         rs, ms = blocks(q, True, phase)
-        if rs:
-            fused([([pc], T.ACC[:, col(r)], T.RL[:, col(r)], "rel%d" % phase, mk) for r, mk in zip(rs, split(mrel(q), len(rs)))])
+        if rs and phase:
+            sl = slice(B * rs[0], B * rs[-1] + B)
+            send(pc, T.RL1[:, sl], T.ACC[:, sl], "rel1", mrel(q))
+        elif rs:
+            fused([([pc], T.ACC[:, col(r)], T.RL[:, col(r)], "rel0", mk) for r, mk in zip(rs, split(mrel(q), len(rs)))])
         rs, ms = blocks(q, False, phase)
         if rs:
             fused([([T.cores[r]], T.ACC[:, col(r)], T.RES[:, col(q)], "res", mk) for r, mk in zip(rs, ms)])
 
     if is0:
-        eY = ev()
-        for k in range(2):
-            cp(T["Y%d" % k][:, 0:1], c_("NEG"), [m2], eY)
-        scn, done = {}, {}
+        scn, done, held = {}, {}, {}
+
+        def take(n):
+            acc, y, xo, d = held[n]
+            done[n] = tt(acc, y[:].indirect(xo), acc, A.max, [scn[n]] + d + ([done[n - 1]] if n else []))
+
         for n, r in enumerate(order_of(q)):
-            X, Y = T["X%d" % (n % 3)], T["Y%d" % (n % 2)]
+            X, Y = T["X%d" % (n % 3)], T["Y%d" % (n % 3)]
             kc, kk = (4 if r in (0, N - 1) else 6), max(0, 2 * r - 2)
             if r == q:
-                off, fl, xo, d1, d2 = T.OUTA[:], T.FLM[:], T.OUTC[:, 0:kc], [eA], [eFM, eC2]
+                off, fl, xo, d1, d2 = T.OUTA[:], T.pE[:], T.OUTC[:, 0:kc], [eA], [eFM, eC2]
             else:
                 off, fl = T.OF[:, 40 * r:40 * r + 32], T.FL[:, CAP * r:CAP * r + CAP]
                 xo = T.OF[:, 40 * r + 32:40 * r + 32 + kc]
                 ne = len(bits(nrep(plans[q][1][r])))
-                d1, d2 = [ext("of%d" % r, ne)], [ext("fl%d" % r, 2 * ne)]
+                d1, d2 = [ext("of%d" % r, ne)], [ext("fl%d" % r, ne), ext("xo%d" % r, ne)]
             ga = do("S", S.activation, (X[:], T.win[:].indirect(off), COPY), tabd + [m2] + d1 + ([scn[n - 3]] if n > 2 else []))
             scn[n] = do("V", V.tensor_tensor_scan, (Y[:, 1:], fl, X[:], c_("NEG"), A.min, A.max),
-                        [ga, m2, eY] + d2 + ([done[n - 2]] if n > 1 else []))
-            acc = T.ACC[:, 16 * kk:16 * kk + 16 * kc]
-            done[n] = tt(acc, Y[:].indirect(xo), acc, A.max, [scn[n]] + ([done[n - 1]] if n else []))
+                        [ga, m2, k2] + d2[:1] + ([done[n - 3]] if n > 2 else []))
+            held[n] = (T.ACC[:, 16 * kk:16 * kk + 16 * kc], Y, xo, d2[1:])
+            for k in range(len(done), n + 1 if n > N - DIRECT else n):
+                take(k)
 
         wait("G", [done[n] for n in range(N - 2)])
         results(0)
@@ -349,11 +378,12 @@ def rank_program(g, core, T, topo):
         results(1)
         fin = cp(T.RES[:, col(q)], T.ACC[:, col(q)], [done[N - 1]])
     if isP:
-        for phase in (0, 1):
+        for phase, RL in ((0, T.RL), (1, T.RL1)):
             rs, ms = blocks(q, True, phase)
             if rs:
-                wait("G", [ext("rel%d" % phase, sum(len(bits(x)) for x in split(mrel(q), len(rs))))])
-                fused([([T.cores[r]], T.RL[:, col(r)], T.RES[:, col(q)], "res", mk) for r, mk in zip(rs, ms)])
+                mks = [mrel(q)] if phase else split(mrel(q), len(rs))
+                wait("G", [ext("rel%d" % phase, sum(len(bits(x)) for x in mks))])
+                fused([([T.cores[r]], RL[:, col(r)], T.RES[:, col(q)], "res", mk) for r, mk in zip(rs, ms)])
     if is0:
         tot = 0
         for k in range(N):
@@ -363,7 +393,7 @@ def rank_program(g, core, T, topo):
         f = tt(T.M[:, 0:128], T.RES[:, 0:128], T.RES[:, 128:256], A.max, [fin, ext("res", tot)])
         f = tt(T.M[:, 128:192], T.M[:, 0:64], T.M[:, 64:128], A.max, [f])
         f3 = tt(T.M[:, 192:224], T.M[:, 128:160], T.M[:, 160:192], A.max, [f])
-        f = ts(T.M[:, 224:256], T.M[:, 192:224], c_("THR"), A.is_le, [f3, m2], None, c_("POS"), A.mult)
+        f = ts(T.M[:, 224:256], T.M[:, 192:224], c_("THR"), A.is_le, [f3, k2], None, c_("POS"), A.mult)
         f = tt(T.M[:, 256:288], T.M[:, 192:224], T.M[:, 224:256], A.add, [f])
         do("Y", SY.dma_start, (T.y[:], T.M[:, 256:288]), [f], None, 16)
     if cnt["ls"]:

from concourse.bass import DstId, RemoteDMATransfer
from concourse.mybir import AluOpType, ActivationFunctionType, AxisListType

N, R, E, B, CAP = 8, 4096, 2048, 32, 512
MID = R // 2
PRE = 1280
NEV = 112
DIRECT = 4
COLS = ["AC", "FC", "WF", "IV", "KV", "T2", "CW", "NEG", "POS", "THR", "CA", "CB", "PC", "F3", "F3b", "F3c"]
SLOT = ["GE", "VW", "VO", "MK", "RK", "PV", "GT", "XO", "S1", "HF", "H16", "KOH", "Z"]

SCRATCH = {"p%s" % k: ("psum", [128, 512], "float32") for k in "ABCDEFG"}
for _t, _l in (("float32", dict(win=R + 1, AF=128, FF=128, MI=128, IDF=96, ONF=128, CREP=128, CSH=128, CWR=128, IOF=128,
                                TB2=128, TA=128, S=16, Q=16 * len(SLOT), ACC=256, RL=256, RL1=256, RES=256, M=288,
                                X0=CAP, X1=CAP, X2=CAP, Y0=CAP + 1, Y1=CAP + 1, Y2=CAP + 1)),
               ("int32", dict(MSG=20, RLY=20, I1=4, I2=48, I3=4)),
               ("uint16", dict(IM=128, IC=32, IOT=CAP, OUTA=32, OUTC=8, OF=40 * N)),
               ("float16", dict(LH=128 * 16, RH=32 * 16, SI=16, OHP=96)),
               ("bfloat16", dict(NB0=128, NB=128, OHF=CAP, FLM=CAP, FL=CAP * N, A1=128, A2=128, A32=128, O=16, INC=16, TB=16,
                                 ON=128, ONB=16, ID=96, DG=96))):
    for _n, _w in _l.items():
        SCRATCH[_n] = ("sbuf", [128, _w], _t)
SEMAPHORES = (["of%d" % h for h in range(N)] + ["fl%d" % h for h in range(N)] + ["xo%d" % h for h in range(N)]
              + ["res", "lm", "lr", "rel0", "rel1", "lsem", "go"] + ["e%d" % k for k in range(NEV)])


def bits(m):
    return [b for b in range(16) if (m >> b) & 1]


def split(mask, n):
    bb = bits(mask)
    k = 1
    while k * 2 * n <= len(bb):
        k *= 2
    return [sum(1 << b for b in bb[i * k:(i + 1) * k]) for i in range(n)]


def common(core, ds, topo):
    m = 0xFFFF
    for d in ds:
        m &= topo.mask(core, d)
    return m


def chip_plan(q, T, topo):
    c0 = T.cores[q]
    cs = [c for c in range(256) if topo.host(c) == topo.host(c0) and topo.chip(c) == topo.chip(c0) and c != c0]
    mate = [c for c in cs if topo.die(c) == topo.die(c0)]
    p = [c for c in mate if all(topo.may_write(c, d) for d in T.cores)][0]
    far = [h for h in range(N) if not topo.may_write(T.cores[h], c0) and h != q]
    nea = [h for h in range(N) if topo.may_write(T.cores[h], c0) and h != q]
    order = [p] + [c for c in mate if c != p] + [c for c in cs if c not in mate]
    return p, dict([(q, c0)] + list(zip(far + nea, order)))


def rank_program(g, core, T, topo):
    plans = [chip_plan(r, T, topo) for r in range(N)]
    ports = [p[0] for p in plans]
    role = [(r, h) for r in range(N) for h in range(N) if plans[r][1][h] == core]
    if not role:
        return
    q, h = role[0]
    c0, pc = T.cores[q], ports[q]
    is0, isP = core == c0, core == pc
    near = lambda r, s: topo.may_write(T.cores[r], T.cores[s])
    A = AluOpType
    COPY = ActivationFunctionType.Copy
    V, S, PE, SY = g.vector, g.scalar, g.tensor, g.sync
    eng = {"V": V, "S": S, "P": PE, "Y": SY, "G": g}
    evs, waited, cnt = [], {}, {"ls": 0}

    def c_(name, P=128, w=1):
        k = COLS.index(name)
        return T.S[0:P, k:k + w]

    def q_(name, a=0, b=16, P=128):
        k = 16 * SLOT.index(name)
        return T.Q[0:P, k + a:k + b]

    def ev():
        e = {"sem": T.sem["e%d" % len(evs)], "n": 0, "k": len(evs)}
        evs.append(e)
        return e

    def ext(name, n):
        return {"sem": T.sem[name], "n": n, "k": name}

    def wait(qn, deps):
        for e in deps:
            key = (qn, e["k"])
            if e["n"] and waited.get(key, 0) < e["n"]:
                eng[qn].wait_ge(e["sem"], e["n"])
                waited[key] = e["n"]

    def do(qn, fn, args, deps, e=None, n=1, **kw):
        wait(qn, deps)
        if e is None:
            e = ev()
        fn(*args, **kw).then_inc(e["sem"], n)
        e["n"] += n
        return e

    def ts(out, i, s1, op, deps, e=None, s2=None, op2=None):
        return do("V", V.tensor_scalar, (out, i, s1, s2, op) + ((op2,) if op2 is not None else ()), deps, e)

    def tt(out, a, b, op, deps, e=None):
        return do("V", V.tensor_tensor, (out, a, b, op), deps, e)

    def cp(out, i, deps, e=None):
        return do("V", V.tensor_copy, (out, i), deps, e)

    def mm(out, l, r, a, b, deps, e=None):
        return do("P", PE.matmul, (out, l, r, a, b), deps, e)

    def iota(ap, pat, base, cm, e):
        do("G", g.iota, (ap, pat, base, cm), [], e, allow_small_or_imprecise_dtypes=True)

    def dst(d):
        rid, pid = topo.addr(d, core)
        return DstId(rid=rid, pnc=pid)

    def send(d, out, in_, sem, mask):
        rid, pid = topo.addr(d, core)
        g.remote_dma(out, in_, T.sem[sem], T.sem.lsem, pid, rid, mask)
        cnt["ls"] += len(bits(mask))

    def fused(trs):
        g.remote_dma_fused([RemoteDMATransfer(dst_ids=[dst(d) for d in ds], dma_engine_mask=mk, remote_sem=T.sem[sem],
                                              srcs=[src], dsts=[out for d in ds]) for ds, src, out, sem, mk in trs],
                           local_sem=T.sem.lsem)
        cnt["ls"] += sum(len(bits(x[4])) for x in trs)

    kin = lambda r: [s for s in range(N) if s == r or near(r, s)]
    turn = lambda r, s: (kin(s).index(s) - kin(r).index(r)) % len(kin(s))
    tabs = lambda r, nr: sorted([s for s in range(N) if s != r and near(r, s) == nr], key=lambda s: turn(r, s))
    tn = lambda r: [plans[s][1][r] for s in tabs(r, True)]
    tf = lambda r: [plans[s][1][r] for s in tabs(r, False)]
    mnear = lambda r: topo.mask(T.cores[r], ports[r]) & common(T.cores[r], tn(r), topo)
    mrel = lambda r: topo.mask(T.cores[r], ports[r]) & ~mnear(r) or mnear(r)

    def order_of(r):
        come = lambda nr: sorted([s for s in range(N) if s != r and near(s, r) == nr], key=lambda s: turn(s, r))
        fr = come(False)
        own = lambda t, nr: len([b for b in range(N) if b != r and near(r, b) == nr and any(abs(b - s) < 2 for s in t)])
        last = min([(a, b) for a in fr for b in fr if fr.index(a) < fr.index(b)],
                   key=lambda t: (own(t, False), own(t, True), -fr.index(t[0]) - fr.index(t[1])))
        return [r] + come(True) + [s for s in fr if s not in last] + list(last)

    def blocks(r, far, phase):
        o = order_of(r)
        late = lambda b: max(o.index(s) for s in (b - 1, b, b + 1) if 0 <= s < N) > N - 3
        rs = [s for s in range(N) if s != r and near(r, s) != far and late(s) == bool(phase)]
        src = ports[r] if far else T.cores[r]
        return (rs, split(common(src, [T.cores[s] for s in rs], topo), len(rs))) if rs else ([], [])

    KC, k0 = (4 if h in (0, N - 1) else 6), max(0, 2 * h - 2)
    W = 16 * KC

    zc = ev()
    if is0:
        eI = do("Y", SY.dma_start, (T.MSG[:, 0:16], T.idx[:]), [], None, 16)
        do("V", V.memset, (T.MSG[:, 16:20], 0), [], zc)
        eE = do("Y", SY.dma_start, (T.MSG[0:W, 16:17], T.end[:, k0:k0 + KC]), [zc], None, 16)
        tabd = [do("Y", SY.dma_start, (T.win[:, 0:PRE], T.tab[:, 0:PRE]), [], None, 16)]
        msgd = [eI, eE, zc]
    else:
        s = T.cores[h] if near(h, q) else ports[h]
        msgd = [ext("lm", len(bits(common(s, tn(h) if near(h, q) else tf(h), topo))))]
    c1, c1b = ev(), ev()
    iota(T.I1[:, 0:1], [[0, 1]], 0, 1, c1)
    iota(T.AF[:], [[0, 16], [1, 8]], 0, 0, c1)
    iota(T.FF[:], [[1, 16], [0, 8]], 0, 0, c1)
    iota(T.MI[:], [[0, 8], [1, 16]], 0, 0, c1)
    iota(c_("WF"), [[0, 1]], 0, 1, c1b)
    if is0:
        wait("G", msgd)
        send(pc, T.RLY[:], T.MSG[:], "lr", mrel(q))
        fused([(tn(q), T.MSG[:], T.MSG[:], "lm", common(core, tn(q), topo))])
        g.sem_inc(T.sem.go, 1)
    iota(T.IDF[0:96, 0:96], [[1, 96]], 0, -1, c1b)
    if isP:
        wait("G", [ext("lr", len(bits(mrel(q))))])
        fused([(tf(q), T.RLY[:], T.MSG[:], "lm", common(core, tf(q), topo))])
    c2 = ev()
    iota(T.IOF[:], [[1, 128]], 0, 0, c2)

    m = ev()
    for ap, v in ((T.ONB[:], 1.0), (T.ON[:], 1.0), (c_("CA"), -9e29), (T.ONF[:], 1.0)):
        do("V", V.memset, (ap, v), [], m)

    def select(out, i, base, up, op, deps, e=None):
        s = 1 if up else -1
        return do("G", g.affine_select, (out, i, [[0, 8], [s * KC, 16]], op, 0.0, base, -s), deps, e)

    c3 = ev()
    x1 = select(T.CREP[0:W, :], T.ONF[0:W, :], KC, True, A.is_gt, [m])
    x2 = select(T.CSH[0:W, :], T.ONF[0:W, :], 0, True, A.is_gt, [m])
    select(T.CWR[0:W, :], T.ONF[0:W, :], -15 * KC, False, A.is_ge, [m], c3)
    select(T.CREP[0:W, :], T.CREP[0:W, :], 0, False, A.is_ge, [x1], c3)
    select(T.CSH[0:W, :], T.CSH[0:W, :], KC, False, A.is_ge, [x2], c3)

    a = ev()
    ts(T.I1[:, 1:2], T.I1[:, 0:1], 7, A.bitwise_and, [c1], a)
    ts(T.I1[:, 2:3], T.I1[:, 0:1], 3, A.arith_shift_right, [c1], a)
    mb = ev()
    for ap, v in ((c_("CW"), 5000.0), (q_("RK"), 0.0), (T.OUTC[:], 0)):
        do("V", V.memset, (ap, v), [], mb)
    b = ev()
    cp(c_("AC"), T.I1[:, 1:2], [a], b)
    cp(c_("FC"), T.I1[:, 2:3], [a], b)
    m2 = ev()
    ts(c_("NEG"), c_("CA"), 2.0, A.mult, [m], m2)
    if is0:
        ts(T.win[:, MID:MID + 1], c_("CA"), 2.0, A.mult, [m], m2)
        wait("Y", [ext("go", 1), m2])
        tabd.append(do("Y", SY.dma_start, (T.win[:, PRE:MID], T.tab[:, PRE:MID]), [], None, 16))
        tabd.append(do("Y", SY.dma_start, (T.win[:, MID + 1:], T.tab[:, MID:]), [], None, 16))
    cst = ev()
    eA2 = ts(T.A2[:], T.AF[:], c_("AC"), A.is_equal, [b])
    e = ts(T.TA[:], T.FF[:], c_("FC"), A.is_gt, [b])
    ts(T.A1[:], T.AF[:], c_("AC"), A.is_gt, [b], cst)
    e = tt(T.TB2[:], T.TA[:], T.A2[:], A.mult, [e, eA2])
    cp(T.IM[:], T.MI[:], [c1], cst)
    cp(T.IC[:, 0:16], T.MI[:, 0:16], [c1], cst)
    ts(T.IC[:, 16:32], T.MI[:, 0:16], 16.0, A.add, [c1], cst)
    tt(T.A32[:], T.TB2[:], T.A2[:], A.subtract, [e], cst)

    k2 = ev()

    def late_constants():
        z = ev()
        for ap, v in ((T.NB0[0:96, :], -9e29), (T.NB0[96:128, :], 1.4e28), (T.IOT[96:128, :], 5000)) + (
                ((T.ACC[:], -9e29), (c_("CB"), -7.5e29)) if is0 else ()):
            do("V", V.memset, (ap, v), [], z)
        e1 = ts(c_("T2"), c_("WF"), 1.0 / KC, A.mult, [c1b], None, -0.5 + 0.5 / KC, A.add)
        i0 = cp(T.IOT[0:96, 0:128], T.IOF[0:96, :], [c2])
        e2 = cp(T.I1[:, 3:4], c_("T2"), [e1])
        ts(T.NB[:], T.NB0[:], 4.0, A.mult, [z], k2)
        e3 = cp(c_("IV"), T.I1[:, 3:4], [e2])
        for k in (1, 2, 3):
            ts(T.IOT[0:96, 128 * k:128 * k + 128], T.IOT[0:96, 0:128], 128.0 * k, A.add, [i0], k2)
        e4 = ts(c_("KV"), c_("IV"), -float(KC), A.mult, [e3], None, c_("WF"), A.add)
        if is0:
            ts(T.ACC[:], T.ACC[:], 2.0, A.mult, [z], k2)
            for k in range(3):
                cp(T["Y%d" % k][:, 0:1], c_("NEG"), [m2], k2)
            ts(c_("POS"), c_("CA"), -2.0, A.mult, [m], k2)
            ts(c_("THR"), c_("CB"), 2.0, A.mult, [z], k2)
        ts(q_("MK", 0, 8), T.IC[:, 0:8], c_("KV"), A.is_equal, [e4, cst], k2)

    if not is0:
        late_constants()
    idd = ts(T.ID[0:96, 0:96], T.IDF[0:96, 0:96], 0.0, A.is_equal, [c1b]) if not is0 else None

    OW, CL, HI = T.I2[:, 0:16], T.I2[:, 16:32], T.I2[:, 32:48]
    wait("V", msgd)
    eOW = ts(OW, T.MSG[:, 0:16], 12, A.arith_shift_right, [])
    eE1 = ts(T.I3[0:W, 3:4], T.MSG[0:W, 16:17], -float(E * h + 1), A.add, [], None, float(E - 1), A.min)
    eCL = ts(CL, T.MSG[:, 0:16], R - 1, A.bitwise_and, [])
    eO = ts(T.O[:], OW, float(q), A.is_equal, [eOW])
    eI3 = ev()
    ts(T.I3[0:W, 0:1], T.I3[0:W, 3:4], 15, A.bitwise_and, [eE1], eI3)
    eIn = do("V", V.tensor_tensor_scan, (T.INC[:], T.ONB[:], T.O[:], 0.0, A.mult, A.add), [eO, m])
    ts(T.I3[0:W, 1:2], T.I3[0:W, 3:4], 8, A.arith_shift_right, [], eI3)
    do("V", V.tensor_scalar, (T.I3[0:W, 2:3], T.I3[0:W, 3:4], 4, 15, A.arith_shift_right, A.bitwise_and), [], eI3)
    eTB = ts(T.TB[:], T.ONB[:], T.INC[:, 15:16], A.mult, [eIn])
    eX = ev()
    mm(T.pA[:, 0:16], T.A2[:], T.INC[:], True, False, [eIn, cst, eA2], eX)
    mm(T.pA[:, 0:16], T.A32[:], T.O[:], False, False, [eO], eX)
    mm(T.pA[:, 0:16], T.A1[:], T.TB[:], False, True, [eTB], eX)
    eF3 = ts(c_("F3", W, 3), T.I3[0:W, 0:3], -0.5, A.max, [eI3])
    eGE = ts(q_("GE"), CL, float(MID), A.is_ge, [eCL], None, -float(MID), A.add)
    if is0:
        idd = ts(T.ID[0:96, 0:96], T.IDF[0:96, 0:96], 0.0, A.is_equal, [c1b])
    ePC = ts(c_("PC", W), c_("F3", W), 8.0, A.mult, [eF3], None, c_("F3b", W), A.add)
    eVW = tt(q_("VW"), CL, q_("GE"), A.add, [eGE])
    eSl = ev()
    ts(HI, T.pA[:, 0:16], -7.5, A.add, [eX], eSl, 1.0 / 16, A.mult)
    cp(q_("S1"), T.pA[:, 0:16], [], eSl)
    eVO = tt(q_("VO"), q_("VW"), T.O[:], A.mult, [eVW])
    eHF = ev()
    cp(q_("HF"), HI, [eSl], eHF)
    ts(q_("H16"), HI, 16.0, A.mult, [], eHF)
    eSI = tt(T.SI[:], T.pA[:, 0:16], T.O[:], A.add, [])
    eDG = ts(T.DG[0:W, 0:W], T.ID[0:W, 0:W], c_("PC", W), A.mult, [ePC, idd])
    ePF = mm(T.pF[:, 0:W], T.ON[0:W, :], T.DG[0:W, 0:W], True, True, [eDG, m])
    eP = ev()
    for k in range(0, 16, 2):
        x = ev()
        for t in (k, k + 1):
            ts(T.LH[:, 128 * t:128 * t + 128], T.IM[:], q_("H16", t, t + 1), A.add, [eHF, cst], x, q_("S1", t, t + 1), A.is_equal)
            ts(T.RH[:, 32 * t:32 * t + 32], T.IC[:], q_("HF", t, t + 1), A.is_equal, [eVO], x, q_("VO", t, t + 1), A.mult)
        for t in (k, k + 1):
            mm(T.pB[:, 0:32], T.LH[:, 128 * t:128 * t + 128], T.RH[:, 32 * t:32 * t + 32], t == 0, t == 15, [x], eP)
        if k == 2:
            oh = ts(T.OHP[:, 0:W], T.pF[:, 0:W], c_("WF"), A.is_equal, [ePF, c1b])
            pk = mm(T.pC[0:W, 0:16], T.OHP[:, 0:W], T.SI[:], True, True, [oh, eSI])
        if k == 6:
            kh = ts(q_("KOH", P=W), T.IC[0:W, 0:16], c_("F3c", W), A.is_equal, [cst])
        if k == 8:
            z = tt(q_("Z", P=W), T.pC[0:W, 0:16], q_("KOH", P=W), A.mult, [pk, kh])
        if k == 10:
            eCW = do("V", V.tensor_reduce, (c_("CW", W), q_("Z", P=W), AxisListType.X, A.add), [z, mb])
    if is0:
        late_constants()
    eFM = ev()
    if is0:
        o = ts(T.OHF[:], T.IOT[:], c_("CW"), A.is_equal, [eCW, k2])
        mm(T.pE[:], T.NB[:], T.OHF[:], True, True, [o], eFM)
    else:
        half = [(slice(0, 256), T.pE[:, 0:256]), (slice(256, 512), T.pG[:, 0:256])]
        for sl, ps in half:
            o = ts(T.OHF[:, sl], T.IOT[:, sl], c_("CW"), A.is_equal, [eCW, k2])
            x = mm(ps, T.NB[:], T.OHF[:, sl], True, True, [o])
            do("S", S.activation, (T.FLM[:, sl], ps, COPY), [x], eFM)
    eA = ts(T.OUTA[:], T.pB[:, 0:32], float(MID), A.add, [eP])
    nrep = lambda c: topo.mask(c, c0) & mnear(q)
    if not is0:
        wait("G", [eA])
        send(c0, T.OF[:, 40 * h:40 * h + 32], T.OUTA[:], "of%d" % h, nrep(core))
    rk, rk1 = q_("RK", 1, 1 + KC, W), q_("RK", 0, KC, W)
    eRK = ts(rk, q_("MK", 0, KC, W), c_("CW", W), A.mult, [eCW, k2, mb])
    eR = ev()
    mm(T.pD[:, 8:8 + KC], T.CSH[0:W, :], rk, True, False, [eRK, c3], eR)
    mm(T.pD[:, 8:8 + KC], T.CWR[0:W, :], rk1, False, True, [], eR)
    mm(T.pD[:, 0:KC], T.CREP[0:W, :], rk, True, True, [], eR)
    e = cp(q_("PV", 0, KC), T.pD[:, 8:8 + KC], [eR])
    e = tt(q_("GT", 0, KC), T.pD[:, 0:KC], q_("PV", 0, KC), A.is_gt, [e])
    e = tt(q_("XO", 0, KC), T.pD[:, 0:KC], q_("GT", 0, KC), A.mult, [e])
    eC2 = cp(T.OUTC[:, 0:KC], q_("XO", 0, KC), [e, mb])
    if not is0:
        wait("G", [eFM])
        send(c0, T.FL[:, CAP * h:CAP * h + CAP], T.FLM[:], "fl%d" % h, nrep(core))
        wait("G", [eC2])
        send(c0, T.OF[:, 40 * h + 32:40 * h + 40], T.OUTC[:], "xo%d" % h, nrep(core))

    col = lambda r: slice(B * r, B * r + B)

    def results(phase):
        rs, ms = blocks(q, True, phase)
        if rs and phase:
            sl = slice(B * rs[0], B * rs[-1] + B)
            send(pc, T.RL1[:, sl], T.ACC[:, sl], "rel1", mrel(q))
        elif rs:
            fused([([pc], T.ACC[:, col(r)], T.RL[:, col(r)], "rel0", mk) for r, mk in zip(rs, split(mrel(q), len(rs)))])
        rs, ms = blocks(q, False, phase)
        if rs:
            fused([([T.cores[r]], T.ACC[:, col(r)], T.RES[:, col(q)], "res", mk) for r, mk in zip(rs, ms)])

    if is0:
        scn, done, held = {}, {}, {}

        def take(n):
            acc, y, xo, d = held[n]
            done[n] = tt(acc, y[:].indirect(xo), acc, A.max, [scn[n]] + d + ([done[n - 1]] if n else []))

        for n, r in enumerate(order_of(q)):
            X, Y = T["X%d" % (n % 3)], T["Y%d" % (n % 3)]
            kc, kk = (4 if r in (0, N - 1) else 6), max(0, 2 * r - 2)
            if r == q:
                off, fl, xo, d1, d2 = T.OUTA[:], T.pE[:], T.OUTC[:, 0:kc], [eA], [eFM, eC2]
            else:
                off, fl = T.OF[:, 40 * r:40 * r + 32], T.FL[:, CAP * r:CAP * r + CAP]
                xo = T.OF[:, 40 * r + 32:40 * r + 32 + kc]
                ne = len(bits(nrep(plans[q][1][r])))
                d1, d2 = [ext("of%d" % r, ne)], [ext("fl%d" % r, ne), ext("xo%d" % r, ne)]
            ga = do("S", S.activation, (X[:], T.win[:].indirect(off), COPY), tabd + [m2] + d1 + ([scn[n - 3]] if n > 2 else []))
            scn[n] = do("V", V.tensor_tensor_scan, (Y[:, 1:], fl, X[:], c_("NEG"), A.min, A.max),
                        [ga, m2, k2] + d2[:1] + ([done[n - 3]] if n > 2 else []))
            held[n] = (T.ACC[:, 16 * kk:16 * kk + 16 * kc], Y, xo, d2[1:])
            for k in range(len(done), n + 1 if n > N - DIRECT else n):
                take(k)

        wait("G", [done[n] for n in range(N - 2)])
        results(0)
        wait("G", [done[N - 2], done[N - 1]])
        results(1)
        fin = cp(T.RES[:, col(q)], T.ACC[:, col(q)], [done[N - 1]])
    if isP:
        for phase, RL in ((0, T.RL), (1, T.RL1)):
            rs, ms = blocks(q, True, phase)
            if rs:
                mks = [mrel(q)] if phase else split(mrel(q), len(rs))
                wait("G", [ext("rel%d" % phase, sum(len(bits(x)) for x in mks))])
                fused([([T.cores[r]], RL[:, col(r)], T.RES[:, col(q)], "res", mk) for r, mk in zip(rs, ms)])
    if is0:
        tot = 0
        for k in range(N):
            for far in (True, False):
                for phase in (0, 1):
                    tot += sum(len(bits(mk)) for r, mk in zip(*blocks(k, far, phase)) if r == q)
        f = tt(T.M[:, 0:128], T.RES[:, 0:128], T.RES[:, 128:256], A.max, [fin, ext("res", tot)])
        f = tt(T.M[:, 128:192], T.M[:, 0:64], T.M[:, 64:128], A.max, [f])
        f3 = tt(T.M[:, 192:224], T.M[:, 128:160], T.M[:, 160:192], A.max, [f])
        f = ts(T.M[:, 224:256], T.M[:, 192:224], c_("THR"), A.is_le, [f3, k2], None, c_("POS"), A.mult)
        f = tt(T.M[:, 256:288], T.M[:, 192:224], T.M[:, 224:256], A.add, [f])
        do("Y", SY.dma_start, (T.y[:], T.M[:, 256:288]), [f], None, 16)
    if cnt["ls"]:
        g.wait_ge(T.sem.lsem, cnt["ls"])
    for e in evs:
        if e["n"] and not any(waited.get((qn, e["k"]), 0) >= e["n"] for qn in eng):
            g.wait_ge(e["sem"], e["n"])
